import numpy as np
import ml_dtypes


def mxq(x, axis, fmt="e4m3"):
    dtype, down = {"e4m3": (ml_dtypes.float8_e4m3fn, 7), "e5m2": (ml_dtypes.float8_e5m2, 14)}[fmt]
    v = np.moveaxis(np.asarray(x, np.float32).astype(ml_dtypes.bfloat16).astype(np.float64), axis, -1)
    blocks = v.reshape(v.shape[:-1] + (-1, 32))
    amax = np.abs(blocks).max(-1, keepdims=True)
    byte = np.maximum(np.where(amax > 0, np.frexp(amax)[1] - 1 + 127, 0) - down, 1)
    scale = np.exp2(byte - 127.0)
    codes = (blocks / scale).astype(np.float32).astype(dtype).astype(np.float64)
    return np.moveaxis((codes * scale).reshape(v.shape), -1, axis)


WIDE = False


def mx_kscale(k):
    if not WIDE:
        return np.ones(k)
    levels = np.array([10, -10, 5, -5, 0])
    if k % 512:
        return np.exp2(np.random.permutation(np.resize(levels, k // 32))).repeat(32)
    a = np.empty((k // 512, 16))
    for p in range(k // 512):
        a[p, :8] = np.random.permutation(np.resize(levels, 8))
        for g in range(8):
            far = levels[np.abs(levels - a[p, g]) >= 10]
            a[p, g + 8] = far[np.random.randint(len(far))]
    return np.exp2(a.ravel()).repeat(32)


BF16 = ml_dtypes.bfloat16


def bf(x):
    return np.asarray(x, np.float32).astype(BF16)


def f64(x):
    return np.asarray(x).astype(np.float64)

E4M3FN = np.array([(-1.0 if i & 128 else 1.0) * ((1.0 + (i & 7) / 8.0) * 2.0 ** (((i >> 3) & 15) - 7) if i & 120 else (i & 7) * 2.0 ** -9) for i in range(256)])


def e4m3fn_bytes(y):
    return np.clip(np.asarray(y, np.float64), -448.0, 448.0).astype(np.float32).astype(ml_dtypes.float8_e4m3fn).view(np.uint8)


def e4m3fn_values(b):
    return E4M3FN[b]


M, N, R, BLK = 2048, 1536, 512, 128
KEEP = 0.9


def setup_inputs():
    s, t = mx_kscale(N), mx_kscale(R)
    a = np.random.standard_normal((R, N)) / np.sqrt(N) / s
    b = np.random.standard_normal((R, N)) / np.sqrt(R) / t[:, None]
    d = {"mom": bf(np.random.standard_normal((M, N)) * s),
         "v": bf((0.3 + 0.7 * np.random.standard_normal((M, R)) ** 2) / (t * t)),
         "w": bf(np.random.standard_normal((M, N)))}
    for name, x in (("a", a), ("b", b)):
        sc = (np.abs(x).reshape(R // BLK, BLK, N // BLK, BLK).max(axis=(1, 3)) / 448.0).astype(np.float32)
        d[name + "_bytes"] = e4m3fn_bytes(x / np.repeat(np.repeat(f64(sc), BLK, axis=0), BLK, axis=1))
        d[name + "_scale"] = sc
    return d


def reference(mom, v, w, a_bytes, a_scale, b_bytes, b_scale):
    a = e4m3fn_values(a_bytes) * np.repeat(np.repeat(f64(a_scale), BLK, axis=0), BLK, axis=1)
    b = e4m3fn_values(b_bytes) * np.repeat(np.repeat(f64(b_scale), BLK, axis=0), BLK, axis=1)
    r = mxq(f64(mom), 1, "e4m3") @ mxq(a, 1, "e4m3").T
    h = r / np.sqrt(f64(v))
    u = mxq(h, 1, "e4m3") @ mxq(b, 0, "e4m3")
    return f64(w) * KEEP - u

@@ -1,0 +1,421 @@
+from contextlib import ExitStack
+
+import concourse.mybir as mybir
+from concourse.masks import make_identity
+
+M, N, R = 2048, 1536, 512
+KEEP = 0.9
+
+FLOPS = 2 * 2 * M * N * R
+
+F32 = mybir.dt.float32
+BF16 = mybir.dt.bfloat16
+U32 = mybir.dt.uint32
+U8 = mybir.dt.uint8
+FP8 = mybir.dt.float8_e4m3fn
+FP8X4 = mybir.dt.float8_e4m3fn_x4
+ALU = mybir.AluOpType
+ACT = mybir.ActivationFunctionType
+
+P = 128
+TILES = M // P
+GROUPS = N // 512
+ROWBLK = R // P
+NBLK = N // P
+CHUNKS = N // 512
+A_BANKS = [("r", "r"), ("r", "r"), ("u", "u"), ("u", "u"), ("u", "u"), ("t", "bank"), ("r", "r"), ("r", "r")]
+
+
+def tile_lowrank_adam_style_step_d7_kernel(
+    tc, mom, v, w, a_bytes, a_scale, b_bytes, b_scale, out
+):
+    nc = tc.nc
+    mom_v = mom.rearrange("(p i) k -> p i k", i=TILES)
+    v_v = v.rearrange("(p i) r -> p i r", i=TILES)
+    w_v = w.rearrange("(p i) n -> p i n", i=TILES)
+    out_v = out.rearrange("(p i) n -> p i n", i=TILES)
+    a_rows = a_bytes.rearrange("(p t) k -> p t k", t=4)
+    b_rows = b_bytes.rearrange("(p t) n -> p t n", t=4)
+
+    with ExitStack() as ctx:
+        keep = ctx.enter_context(tc.tile_pool(name="keep", bufs=1))
+        momp = ctx.enter_context(tc.tile_pool(name="momp", bufs=6))
+        wp = ctx.enter_context(tc.tile_pool(name="wp", bufs=8))
+        widep = ctx.enter_context(tc.tile_pool(name="widep", bufs=4))
+        bp = ctx.enter_context(tc.tile_pool(name="bp", bufs=2))
+        hqp = ctx.enter_context(tc.tile_pool(name="hqp", bufs=8))
+        work = ctx.enter_context(tc.tile_pool(name="work", bufs=3))
+        shp = ctx.enter_context(tc.tile_pool(name="shp", bufs=2))
+        rsp = ctx.enter_context(tc.tile_pool(name="rsp", bufs=5))
+        outp = ctx.enter_context(tc.tile_pool(name="outp", bufs=14))
+        ps_tr = ctx.enter_context(tc.psum_pool(name="ps_tr", bufs=3))
+        ps_r = ctx.enter_context(tc.psum_pool(name="ps_r", bufs=2))
+        ps_u = ctx.enter_context(tc.psum_pool(name="ps_u", bufs=3))
+        ctx.enter_context(tc.manual_schedule())
+
+        warm = keep.tile([P, 1], F32)
+        nc.vector.memset(warm[:], 1.0)
+        warm_o = keep.tile([P, 1], F32)
+        a_sc = keep.tile([P, NBLK], F32)
+        b_sc = keep.tile([P, NBLK], F32)
+        a_all = keep.tile([P, ROWBLK * NBLK], F32)
+        b_all = keep.tile([P, ROWBLK * NBLK], F32)
+        nc.scalar.dma_start(out=a_all[:], in_=a_scale.rearrange("i j -> (i j)").partition_broadcast(P))
+        nc.scalar.dma_start(out=b_all[:], in_=b_scale.rearrange("i j -> (i j)").partition_broadcast(P))
+        for q in range(4):
+            rows = slice(32 * q, 32 * q + 32)
+            nc.vector.tensor_copy(out=a_sc[rows], in_=a_all[rows, NBLK * q : NBLK * (q + 1)])
+        nc.scalar.activation(out=warm_o[:], in_=warm[:], func=ACT.Abs_reciprocal_sqrt)
+        ident = keep.tile([P, P], F32)
+        make_identity(nc, ident[:])
+        for q in range(4):
+            rows = slice(32 * q, 32 * q + 32)
+            nc.gpsimd.tensor_copy(out=b_sc[rows], in_=b_all[rows, NBLK * q : NBLK * (q + 1)])
+
+        mom_t, v_t, w_t, o_t = {}, {}, {}, {}
+        a_b = keep.tile([P, 4, N], U8)
+        b_b = [keep.tile([P, 4, 512], U8, name="b_b%d" % c) for c in range(CHUNKS)]
+
+        def load_a(t):
+            nc.sync.dma_start(out=a_b[:, t, :], in_=a_rows[:, t, :])
+
+        def load_b(c):
+            nc.sync.dma_start(out=b_b[c][:], in_=b_rows[:, :, 512 * c : 512 * (c + 1)])
+
+        def load_mom(k, n=2):
+            if k % 2 == 0:
+                mom_t[k] = momp.tile([P, 2, N], BF16, name="mom_t")
+                mom_t[k + 1] = mom_t[k]
+            h = k % 2
+            nc.sync.dma_start(out=mom_t[k][:, h : h + n, :], in_=mom_v[:, k : k + n, :])
+
+        def load_v(j):
+            vt = keep.tile([P, 4, R], BF16, name="v_t%d" % j)
+            nc.sync.dma_start(out=vt[:], in_=v_v[:, 4 * j : 4 * j + 4, :])
+            v_t[j] = vt
+
+        def load_w(k):
+            wt = wp.tile([P, 2, N], BF16, name="w_t")
+            nc.sync.dma_start(out=wt[:], in_=w_v[:, k : k + 2, :])
+            w_t[k] = w_t[k + 1] = wt
+
+        def cast(e, dst, src):
+            if e == "S":
+                nc.scalar.copy(out=dst, in_=src)
+            else:
+                nc.vector.tensor_copy(out=dst, in_=src)
+
+        def scaled(e, dst, src, sc):
+            if e == "S":
+                nc.scalar.activation(out=dst, in_=src, func=ACT.Copy, scale=sc)
+            else:
+                nc.vector.tensor_scalar(out=dst, in0=src, scalar1=sc, scalar2=None, op0=ALU.mult)
+
+        a_g = keep.tile([P, GROUPS, 4 * R], BF16, align_bytes=64)
+        a_c = keep.tile([P, GROUPS, R], U32, align_bytes=64)
+        a_s = keep.tile([P, GROUPS, R], U8, align_bytes=64)
+        a_words = a_g[:].bitcast(F32).rearrange("p g (m u) -> p g m u", u=2)
+        a_wide, a_bank = {}, {}
+
+        def scale_a(t, js, e):
+            if t not in a_wide:
+                a_wide[t] = widep.tile([P, N], BF16, name="wide")
+            for j in js:
+                cols = slice(P * j, P * (j + 1))
+                scaled(e, a_wide[t][:, cols], a_b[:, t, cols].bitcast(FP8), a_sc[:, j : j + 1])
+
+        def turn_a(t, bs=(0, 1)):
+            words = a_wide[t][:].bitcast(F32)
+            for b in bs:
+                g0, g1 = ((0, 2), (2, 3))[b]
+                pool, name = A_BANKS[2 * t + b]
+                bank = {"t": ps_tr, "r": ps_r, "u": ps_u}[pool].tile([P, 4, P], F32, name=name)
+                a_bank[t, b] = bank
+                for g in range(g0, g1):
+                    for u in range(2):
+                        nc.tensor.transpose(
+                            bank[:, 2 * (g - g0) + u, :],
+                            words[:, 256 * g + u : 256 * (g + 1) : 2],
+                            ident[:],
+                        )
+
+        def empty_a(t, b, e):
+            g0, g1 = ((0, 2), (2, 3))[b]
+            cast(
+                e,
+                a_words[:, g0:g1, P * t : P * (t + 1), :],
+                a_bank[t, b][:, 0 : 2 * (g1 - g0), :].rearrange("p (g u) m -> p g m u", u=2),
+            )
+
+        def quant_a(g):
+            nc.vector.quantize_mx(
+                out=a_c[:, g, :].bitcast(FP8X4), scales=a_s[:, g, :], in_=a_g[:, g, :]
+            )
+
+        b_c = keep.tile([P, N], U32, align_bytes=64)
+        b_s = keep.tile([P, N], U8, align_bytes=64)
+        b_wide, b_g = {}, {}
+
+        def widen_b(c, t0, t1, e):
+            if c not in b_wide:
+                b_wide[c] = bp.tile([P, 4, 512], BF16, name="b_wide")
+            cast(
+                e,
+                b_wide[c][:, t0:t1, :].rearrange("p t n -> p (t n)"),
+                b_b[c][:, t0:t1, :].rearrange("p t n -> p (t n)").bitcast(FP8),
+            )
+
+        def scale_b(c, js, e):
+            if c not in b_g:
+                b_g[c] = bp.tile([P, 512, 4], BF16, align_bytes=64, name="b_g")
+            for j in js:
+                cols = slice(P * j, P * (j + 1))
+                jj = 4 * c + j
+                scaled(e, b_g[c][:, cols, :], b_wide[c][:, :, cols].rearrange("p t n -> p n t"), b_sc[:, jj : jj + 1])
+
+        def quant_b(c):
+            cols = slice(512 * c, 512 * (c + 1))
+            nc.vector.quantize_mx(
+                out=b_c[:, cols].bitcast(FP8X4),
+                scales=b_s[:, cols],
+                in_=b_g[c][:].rearrange("p n t -> p (n t)"),
+            )
+
+        st = {k: {} for k in range(TILES)}
+
+        def shuffle(k):
+            words = mom_t[k][:, k % 2, :].bitcast(F32)
+            vwords = v_t[k // 4][:, k % 4, :].bitcast(F32)
+            sh = shp.tile([P, 4, P], F32, name="sh")
+            nc.scalar.copy(out=sh[:, 0:2, :], in_=words[:, 512:768].rearrange("p (n u) -> p u n", u=2))
+            nc.scalar.copy(out=sh[:, 2:4, :], in_=vwords.rearrange("p (n u) -> p u n", u=2))
+            st[k]["sh"] = sh
+
+        def turn(k):
+            words = mom_t[k][:, k % 2, :].bitcast(F32)
+            vwords = v_t[k // 4][:, k % 4, :].bitcast(F32)
+            bx = ps_tr.tile([P, 4, P], F32, name="bank")
+            for g in range(2):
+                for u in range(2):
+                    nc.tensor.transpose(
+                        bx[:, 2 * g + u, :], words[:, 256 * g + u : 256 * (g + 1) : 2], ident[:]
+                    )
+            by = ps_tr.tile([P, 4, P], F32, name="bank")
+            for u in range(2):
+                nc.tensor.transpose(
+                    by[:, u, :], st[k]["sh"][:, u, :] if "sh" in st[k] else words[:, 512 + u : 768 : 2], ident[:]
+                )
+            for u in range(2):
+                nc.tensor.transpose(
+                    by[:, 2 + u, :], st[k]["sh"][:, 2 + u, :] if "sh" in st[k] else vwords[:, u::2], ident[:]
+                )
+            st[k]["bx"], st[k]["by"] = bx, by
+
+        def empty(k):
+            bx, by = st[k]["bx"], st[k]["by"]
+            mg = work.tile([P, GROUPS, 4 * P], BF16, align_bytes=64, name="mg")
+            mg_words = mg[:].bitcast(F32)
+            nc.scalar.copy(
+                out=mg_words[:, 0:2, :].rearrange("p g (n u) -> p g n u", u=2),
+                in_=bx[:].rearrange("p (g u) n -> p g n u", u=2),
+            )
+            nc.scalar.copy(
+                out=mg_words[:, 2, :].rearrange("p (n u) -> p n u", u=2),
+                in_=by[:, 0:2, :].rearrange("p u n -> p n u"),
+            )
+            rs = rsp.tile([P, P, 2, 2], F32, name="rs")
+            nc.scalar.activation(
+                out=rs[:],
+                in_=by[:, 2:4, :].bitcast(BF16).rearrange("p u (n e) -> p n u e", e=2),
+                func=ACT.Abs_reciprocal_sqrt,
+            )
+            st[k]["mg"], st[k]["rs"] = mg, rs
+
+        def quant_mom(k, parts=(0, 1)):
+            mg = st[k]["mg"]
+            if 0 in parts:
+                st[k]["mc"] = work.tile([P, GROUPS, P], U32, align_bytes=64, name="mc")
+                st[k]["ms"] = work.tile([P, GROUPS, P], U8, align_bytes=64, name="ms")
+            mc, ms = st[k]["mc"], st[k]["ms"]
+            for g0, g1 in [((0, 2), (2, 3))[x] for x in parts]:
+                nc.vector.quantize_mx(
+                    out=mc[:, g0:g1, :].rearrange("p g n -> p (g n)").bitcast(FP8X4),
+                    scales=ms[:, g0:g1, :].rearrange("p g n -> p (g n)"),
+                    in_=mg[:, g0:g1, :].rearrange("p g n -> p (g n)"),
+                )
+
+        def project(k, t):
+            mc, ms = st[k]["mc"], st[k]["ms"]
+            if t == 0:
+                st[k]["r"] = ps_r.tile([P, 4, P], F32, name="r")
+            for g in range(GROUPS):
+                nc.tensor.matmul_mx(
+                    out=st[k]["r"][:, t, :],
+                    lhsT=a_c[:, g, P * t : P * (t + 1)].bitcast(FP8X4),
+                    lhsT_scale=a_s[:, g, P * t : P * (t + 1)],
+                    rhs=mc[:, g, :].bitcast(FP8X4),
+                    rhs_scale=ms[:, g, :],
+                    start=(g == 0),
+                    stop=(g == GROUPS - 1),
+                )
+
+        def direction(k):
+            h = work.tile([P, P, 4], BF16, align_bytes=64, name="h")
+            nc.vector.tensor_tensor(
+                out=h[:],
+                in0=st[k]["r"][:].rearrange("p t n -> p n t"),
+                in1=st[k]["rs"][:].rearrange("p n u e -> p n (u e)"),
+                op=ALU.mult,
+            )
+            st[k]["h"] = h
+
+        def quant_h(k):
+            hc = hqp.tile([P, P], U32, align_bytes=64, name="hc")
+            hs = hqp.tile([P, P], U8, align_bytes=64, name="hs")
+            nc.vector.quantize_mx(
+                out=hc[:].bitcast(FP8X4),
+                scales=hs[:],
+                in_=st[k]["h"][:].rearrange("p n t -> p (n t)"),
+            )
+            st[k]["hc"], st[k]["hs"] = hc, hs
+
+        u_bank = {}
+
+        def lift(k, c):
+            cols = slice(512 * c, 512 * (c + 1))
+            u = ps_u.tile([P, 4, P], F32, name="u")
+            nc.tensor.matmul_mx(
+                out=u[:].rearrange("p a b -> p (a b)"),
+                lhsT=st[k]["hc"][:].bitcast(FP8X4),
+                lhsT_scale=st[k]["hs"][:],
+                rhs=b_c[:, cols].bitcast(FP8X4),
+                rhs_scale=b_s[:, cols],
+                start=True,
+                stop=True,
+            )
+            u_bank[k, c] = u
+
+        def finish(k, c):
+            cols = slice(512 * c, 512 * (c + 1))
+            o = outp.tile([P, 512], F32, name="o")
+            nc.vector.scalar_tensor_tensor(
+                out=o[:],
+                in0=w_t[k][:, k % 2, cols],
+                scalar=KEEP,
+                in1=u_bank[k, c][:].rearrange("p a b -> p (a b)"),
+                op0=ALU.mult,
+                op1=ALU.subtract,
+            )
+            nc.sync.dma_start(out=out_v[:, k, cols], in_=o[:])
+
+        for t in range(4):
+            load_a(t)
+        load_mom(0, 1)
+        load_b(0)
+        load_v(0)
+        load_mom(1, 1)
+        load_mom(2)
+        load_b(1)
+        load_w(0)
+        load_b(2)
+        load_mom(4)
+        load_v(1)
+        load_w(2)
+        load_mom(6)
+        load_v(2)
+        load_mom(8)
+        load_w(4)
+        more = [(load_mom, 10), (load_w, 6), (load_v, 3), (load_mom, 12), (load_w, 8), (load_mom, 14), (load_w, 10), (load_w, 12), (load_w, 14)]
+
+        V_J, S_J = range(0, 8), range(8, 12)
+        scale_a(0, V_J, "V")
+        scale_a(0, S_J, "S")
+        turn_a(0)
+        scale_a(1, V_J, "V")
+        scale_a(1, S_J, "S")
+        turn_a(1)
+        scale_a(2, V_J, "V")
+        empty_a(0, 0, "S")
+        scale_a(2, S_J, "S")
+        turn_a(2)
+        empty_a(0, 1, "V")
+        scale_a(3, V_J, "V")
+        empty_a(1, 0, "S")
+        scale_a(3, S_J, "S")
+        turn_a(3)
+        turn(0)
+        empty_a(1, 1, "V")
+        empty_a(2, 1, "V")
+        empty_a(2, 0, "S")
+        empty_a(3, 0, "V")
+        empty_a(3, 1, "V")
+        empty(0)
+        turn(1)
+        empty(1)
+        quant_a(0)
+        quant_a(1)
+        quant_a(2)
+
+        queue, outstanding = [], []
+        allowed = {0}
+
+        def next_final():
+            for x in queue:
+                if x[1] in allowed:
+                    queue.remove(x)
+                    return x
+            return None
+
+        def step(s, n, ev=(), es=(), sh=False):
+            ev, es = list(ev), list(es)
+            if sh and s + 4 < TILES:
+                shuffle(s + 4)
+            if s + 3 < TILES:
+                turn(s + 3)
+            vec = [lambda: direction(s), lambda: quant_mom(s + 2), lambda: quant_h(s), lambda: None]
+            on = [s < TILES, s + 2 < TILES, s < TILES, False]
+            for i in range(4):
+                if outstanding and (i < 3 or n > 3):
+                    finish(*outstanding.pop(0))
+                if s + 1 < TILES:
+                    project(s + 1, i)
+                if i < n:
+                    x = next_final()
+                    if x is not None:
+                        lift(*x)
+                        outstanding.append(x)
+                if on[i]:
+                    vec[i]()
+                if ev:
+                    ev.pop(0)()
+            for f in ev:
+                f()
+            if s + 3 < TILES:
+                empty(s + 3)
+            for f in es:
+                f()
+            if s < TILES:
+                queue.extend((s, c) for c in range(CHUNKS))
+            if more:
+                f, a = more.pop(0)
+                f(a)
+        quant_mom(0)
+        widen_b(0, 0, 4, "V")
+        for t in range(4):
+            project(0, t)
+        turn(2)
+        scale_b(0, (0, 1, 2, 3), "V")
+        quant_mom(1)
+        quant_b(0)
+        empty(2)
+
+        step(0, 0, (lambda: widen_b(1, 0, 4, "V"), lambda: scale_b(1, (0, 1), "V")), (lambda: scale_b(1, (2, 3), "S"),))
+        step(1, 1, (lambda: quant_b(1),), (lambda: widen_b(2, 0, 4, "S"),))
+        allowed.add(1)
+        step(2, 2, (lambda: scale_b(2, (0, 1), "V"),), (lambda: scale_b(2, (2, 3), "S"),))
+        step(3, 3, (lambda: quant_b(2),))
+        allowed.add(2)
+        for s in range(4, TILES):
+            step(s, 4 if len(queue) > 4 else 3, sh=True)
+        while queue or outstanding:
+            step(TILES, 3)

@@ -56,21 +56,21 @@ def tile_lowrank_adam_style_step_d7_kernel(
         warm = keep.tile([P, 1], F32)
         nc.vector.memset(warm[:], 1.0)
         warm_o = keep.tile([P, 1], F32)
-        a_sc = keep.tile([P, NBLK], F32)
-        b_sc = keep.tile([P, NBLK], F32)
-        a_all = keep.tile([P, ROWBLK * NBLK], F32)
-        b_all = keep.tile([P, ROWBLK * NBLK], F32)
-        nc.scalar.dma_start(out=a_all[:], in_=a_scale.rearrange("i j -> (i j)").partition_broadcast(P))
-        nc.scalar.dma_start(out=b_all[:], in_=b_scale.rearrange("i j -> (i j)").partition_broadcast(P))
-        for q in range(4):
-            rows = slice(32 * q, 32 * q + 32)
-            nc.vector.tensor_copy(out=a_sc[rows], in_=a_all[rows, NBLK * q : NBLK * (q + 1)])
+        sc_rows = keep.tile([P, 32], F32, align_bytes=64)
+        sc_cols = keep.tile([P, 32], F32, align_bytes=64)
+        sc_wide = keep.tile([P, 32], F32, align_bytes=64)
+        sc_all = keep.tile([P, 32], F32, align_bytes=64)
+        nc.vector.memset(sc_rows[:], 0.0)
+        nc.scalar.dma_start(out=sc_rows[0:P:32, 0:NBLK], in_=a_scale)
+        nc.scalar.dma_start(out=sc_rows[0:P:32, 16 : 16 + NBLK], in_=b_scale)
         nc.scalar.activation(out=warm_o[:], in_=warm[:], func=ACT.Abs_reciprocal_sqrt)
+        nc.vector.transpose(out=sc_cols[:], in_=sc_rows[:])
+        nc.vector.tensor_copy(out=sc_wide[:], in_=sc_cols[:, 0:1].to_broadcast([P, 32]))
+        nc.vector.transpose(out=sc_all[:], in_=sc_wide[:])
+        a_sc = sc_all[:, 0:NBLK]
+        b_sc = sc_all[:, 16 : 16 + NBLK]
         ident = keep.tile([P, P], F32)
         make_identity(nc, ident[:])
-        for q in range(4):
-            rows = slice(32 * q, 32 * q + 32)
-            nc.gpsimd.tensor_copy(out=b_sc[rows], in_=b_all[rows, NBLK * q : NBLK * (q + 1)])
 
         mom_t, v_t, w_t, o_t = {}, {}, {}, {}
         a_b = keep.tile([P, 4, N], U8)

@@ -20,10 +20,10 @@ ACT = mybir.ActivationFunctionType
 P = 128
 TILES = M // P
 GROUPS = N // 512
-ROWBLK = R // P
 NBLK = N // P
 CHUNKS = N // 512
-A_BANKS = [("r", "r"), ("r", "r"), ("u", "u"), ("u", "u"), ("u", "u"), ("t", "bank"), ("r", "r"), ("r", "r")]
+SORTED = 2
+A_ON_VECTOR = 8
 
 
 def tile_lowrank_adam_style_step_d7_kernel(
@@ -39,31 +39,24 @@ def tile_lowrank_adam_style_step_d7_kernel(
 
     with ExitStack() as ctx:
         keep = ctx.enter_context(tc.tile_pool(name="keep", bufs=1))
-        momp = ctx.enter_context(tc.tile_pool(name="momp", bufs=6))
-        wp = ctx.enter_context(tc.tile_pool(name="wp", bufs=8))
-        widep = ctx.enter_context(tc.tile_pool(name="widep", bufs=4))
-        bp = ctx.enter_context(tc.tile_pool(name="bp", bufs=2))
-        hqp = ctx.enter_context(tc.tile_pool(name="hqp", bufs=8))
-        work = ctx.enter_context(tc.tile_pool(name="work", bufs=3))
-        shp = ctx.enter_context(tc.tile_pool(name="shp", bufs=2))
-        rsp = ctx.enter_context(tc.tile_pool(name="rsp", bufs=5))
-        outp = ctx.enter_context(tc.tile_pool(name="outp", bufs=14))
-        ps_tr = ctx.enter_context(tc.psum_pool(name="ps_tr", bufs=3))
+        big = ctx.enter_context(tc.tile_pool(name="big", bufs=19))
+        groupp = ctx.enter_context(tc.tile_pool(name="groupp", bufs=4))
+        qinp = ctx.enter_context(tc.tile_pool(name="qinp", bufs=3))
+        qoutp = ctx.enter_context(tc.tile_pool(name="qoutp", bufs=3))
+        small = ctx.enter_context(tc.tile_pool(name="small", bufs=2))
+        rsp = ctx.enter_context(tc.tile_pool(name="rsp", bufs=3))
+        ps_t = ctx.enter_context(tc.psum_pool(name="ps_t", bufs=3))
         ps_r = ctx.enter_context(tc.psum_pool(name="ps_r", bufs=2))
         ps_u = ctx.enter_context(tc.psum_pool(name="ps_u", bufs=3))
         ctx.enter_context(tc.manual_schedule())
 
-        warm = keep.tile([P, 1], F32)
-        nc.vector.memset(warm[:], 1.0)
-        warm_o = keep.tile([P, 1], F32)
         sc_rows = keep.tile([P, 32], F32, align_bytes=64)
         sc_cols = keep.tile([P, 32], F32, align_bytes=64)
         sc_wide = keep.tile([P, 32], F32, align_bytes=64)
         sc_all = keep.tile([P, 32], F32, align_bytes=64)
-        nc.vector.memset(sc_rows[:], 0.0)
+        nc.gpsimd.memset(sc_rows[:], 0.0)
         nc.scalar.dma_start(out=sc_rows[0:P:32, 0:NBLK], in_=a_scale)
         nc.scalar.dma_start(out=sc_rows[0:P:32, 16 : 16 + NBLK], in_=b_scale)
-        nc.scalar.activation(out=warm_o[:], in_=warm[:], func=ACT.Abs_reciprocal_sqrt)
         nc.vector.transpose(out=sc_cols[:], in_=sc_rows[:])
         nc.vector.tensor_copy(out=sc_wide[:], in_=sc_cols[:, 0:1].to_broadcast([P, 32]))
         nc.vector.transpose(out=sc_all[:], in_=sc_wide[:])
@@ -73,105 +66,107 @@ def tile_lowrank_adam_style_step_d7_kernel(
         make_identity(nc, ident[:])
 
         mom_t, v_t, w_t, o_t = {}, {}, {}, {}
-        a_b = keep.tile([P, 4, N], U8)
-        b_b = [keep.tile([P, 4, 512], U8, name="b_b%d" % c) for c in range(CHUNKS)]
+        a_b = [keep.tile([P, N], U8, name="a_b%d" % t) for t in range(4)]
+        b_b = [keep.tile([P, 2, N], U8, name="b_b%d" % x) for x in range(2)]
 
         def load_a(t):
-            nc.sync.dma_start(out=a_b[:, t, :], in_=a_rows[:, t, :])
+            nc.sync.dma_start(out=a_b[t][:], in_=a_rows[:, t, :])
 
-        def load_b(c):
-            nc.sync.dma_start(out=b_b[c][:], in_=b_rows[:, :, 512 * c : 512 * (c + 1)])
+        def load_b(x):
+            nc.sync.dma_start(out=b_b[x][:], in_=b_rows[:, 2 * x : 2 * x + 2, :])
 
-        def load_mom(k, n=2):
-            if k % 2 == 0:
-                mom_t[k] = momp.tile([P, 2, N], BF16, name="mom_t")
-                mom_t[k + 1] = mom_t[k]
-            h = k % 2
-            nc.sync.dma_start(out=mom_t[k][:, h : h + n, :], in_=mom_v[:, k : k + n, :])
+        def load_mom(k):
+            pair = big.tile([P, 2, N], BF16, name="mom_pair", tag="big")
+            nc.sync.dma_start(out=pair[:], in_=mom_v[:, k : k + 2, :])
+            mom_t[k], mom_t[k + 1] = pair[:, 0, :], pair[:, 1, :]
 
-        def load_v(j):
-            vt = keep.tile([P, 4, R], BF16, name="v_t%d" % j)
-            nc.sync.dma_start(out=vt[:], in_=v_v[:, 4 * j : 4 * j + 4, :])
-            v_t[j] = vt
+        def load_mom_single(k):
+            one = keep.tile([P, N], BF16, name="mom_one%d" % k)
+            nc.sync.dma_start(out=one[:], in_=mom_v[:, k, :])
+            mom_t[k] = one[:]
+
+        def load_v(k, n):
+            vt = keep.tile([P, n, R], BF16, name="v_t%d" % k)
+            nc.sync.dma_start(out=vt[:], in_=v_v[:, k : k + n, :])
+            for i in range(n):
+                v_t[k + i] = vt[:, i, :]
 
         def load_w(k):
-            wt = wp.tile([P, 2, N], BF16, name="w_t")
-            nc.sync.dma_start(out=wt[:], in_=w_v[:, k : k + 2, :])
-            w_t[k] = w_t[k + 1] = wt
+            pair = big.tile([P, 2, N], BF16, name="w_pair", tag="big")
+            nc.sync.dma_start(out=pair[:], in_=w_v[:, k : k + 2, :])
+            w_t[k], w_t[k + 1] = pair[:, 0, :], pair[:, 1, :]
 
-        def cast(e, dst, src):
-            if e == "S":
+        def move(eng, dst, src):
+            if eng == "S":
                 nc.scalar.copy(out=dst, in_=src)
             else:
                 nc.vector.tensor_copy(out=dst, in_=src)
 
-        def scaled(e, dst, src, sc):
-            if e == "S":
+        def scaled(eng, dst, src, sc):
+            if eng == "S":
                 nc.scalar.activation(out=dst, in_=src, func=ACT.Copy, scale=sc)
             else:
                 nc.vector.tensor_scalar(out=dst, in0=src, scalar1=sc, scalar2=None, op0=ALU.mult)
 
-        a_g = keep.tile([P, GROUPS, 4 * R], BF16, align_bytes=64)
+        a_wide = [keep.tile([P, N], BF16, name="a_wide%d" % t) for t in range(4)]
         a_c = keep.tile([P, GROUPS, R], U32, align_bytes=64)
         a_s = keep.tile([P, GROUPS, R], U8, align_bytes=64)
-        a_words = a_g[:].bitcast(F32).rearrange("p g (m u) -> p g m u", u=2)
-        a_wide, a_bank = {}, {}
+        a_g, a_bank = {}, {}
 
-        def scale_a(t, js, e):
-            if t not in a_wide:
-                a_wide[t] = widep.tile([P, N], BF16, name="wide")
-            for j in js:
+        def widen_a(t):
+            for j in range(NBLK):
                 cols = slice(P * j, P * (j + 1))
-                scaled(e, a_wide[t][:, cols], a_b[:, t, cols].bitcast(FP8), a_sc[:, j : j + 1])
+                eng = "V" if j < A_ON_VECTOR else "S"
+                scaled(eng, a_wide[t][:, cols], a_b[t][:, cols].bitcast(FP8), a_sc[:, j : j + 1])
 
-        def turn_a(t, bs=(0, 1)):
+        def turn_a(t):
+            u, e = divmod(t, 2)
             words = a_wide[t][:].bitcast(F32)
-            for b in bs:
-                g0, g1 = ((0, 2), (2, 3))[b]
-                pool, name = A_BANKS[2 * t + b]
-                bank = {"t": ps_tr, "r": ps_r, "u": ps_u}[pool].tile([P, 4, P], F32, name=name)
-                a_bank[t, b] = bank
-                for g in range(g0, g1):
-                    for u in range(2):
-                        nc.tensor.transpose(
-                            bank[:, 2 * (g - g0) + u, :],
-                            words[:, 256 * g + u : 256 * (g + 1) : 2],
-                            ident[:],
-                        )
+            for g in range(GROUPS):
+                if e == 0:
+                    if u == 0:
+                        a_bank[g, u] = ps_u.tile([P, 4, P], F32, name="u")
+                    elif g < 2:
+                        a_bank[g, u] = ps_r.tile([P, 4, P], F32, name="r")
+                    else:
+                        a_bank[g, u] = ps_t.tile([P, 4, P], F32, name="bank")
+                for x in range(2):
+                    nc.tensor.transpose(
+                        a_bank[g, u][:, 2 * e + x, :], words[:, 256 * g + x : 256 * (g + 1) : 2], ident[:]
+                    )
 
-        def empty_a(t, b, e):
-            g0, g1 = ((0, 2), (2, 3))[b]
-            cast(
-                e,
-                a_words[:, g0:g1, P * t : P * (t + 1), :],
-                a_bank[t, b][:, 0 : 2 * (g1 - g0), :].rearrange("p (g u) m -> p g m u", u=2),
+        def empty_a(g, u, eng):
+            if g not in a_g:
+                a_g[g] = groupp.tile([P, 4 * R], BF16, align_bytes=64, name="a_g", tag="group")
+            words = a_g[g][:].bitcast(F32)
+            move(
+                eng,
+                words[:, 512 * u : 512 * (u + 1)].rearrange("p (m y) -> p m y", y=4),
+                a_bank[g, u][:].rearrange("p y m -> p m y"),
             )
 
         def quant_a(g):
-            nc.vector.quantize_mx(
-                out=a_c[:, g, :].bitcast(FP8X4), scales=a_s[:, g, :], in_=a_g[:, g, :]
-            )
+            nc.vector.quantize_mx(out=a_c[:, g, :].bitcast(FP8X4), scales=a_s[:, g, :], in_=a_g[g][:])
 
+        b_wide = keep.tile([P, 4, N], BF16)
         b_c = keep.tile([P, N], U32, align_bytes=64)
         b_s = keep.tile([P, N], U8, align_bytes=64)
-        b_wide, b_g = {}, {}
+        b_g = {}
 
-        def widen_b(c, t0, t1, e):
-            if c not in b_wide:
-                b_wide[c] = bp.tile([P, 4, 512], BF16, name="b_wide")
-            cast(
-                e,
-                b_wide[c][:, t0:t1, :].rearrange("p t n -> p (t n)"),
-                b_b[c][:, t0:t1, :].rearrange("p t n -> p (t n)").bitcast(FP8),
-            )
+        def widen_b(t, eng):
+            move(eng, b_wide[:, t, :], b_b[t // 2][:, t % 2, :].bitcast(FP8))
 
-        def scale_b(c, js, e):
+        def scale_b(c, js, eng):
             if c not in b_g:
-                b_g[c] = bp.tile([P, 512, 4], BF16, align_bytes=64, name="b_g")
+                b_g[c] = groupp.tile([P, 512, 4], BF16, align_bytes=64, name="b_g", tag="group")
             for j in js:
-                cols = slice(P * j, P * (j + 1))
                 jj = 4 * c + j
-                scaled(e, b_g[c][:, cols, :], b_wide[c][:, :, cols].rearrange("p t n -> p n t"), b_sc[:, jj : jj + 1])
+                scaled(
+                    eng,
+                    b_g[c][:, P * j : P * (j + 1), :],
+                    b_wide[:, :, P * jj : P * (jj + 1)].rearrange("p t n -> p n t"),
+                    b_sc[:, jj : jj + 1],
+                )
 
         def quant_b(c):
             cols = slice(512 * c, 512 * (c + 1))
@@ -181,241 +176,202 @@ def tile_lowrank_adam_style_step_d7_kernel(
                 in_=b_g[c][:].rearrange("p n t -> p (n t)"),
             )
 
-        st = {k: {} for k in range(TILES)}
+        srt, rs, h, r_bank, u_bank = {}, {}, {}, {}, {}
+        bank_x, bank_y, q_in, q_c, q_s = {}, {}, {}, {}, {}
 
-        def shuffle(k):
-            words = mom_t[k][:, k % 2, :].bitcast(F32)
-            vwords = v_t[k // 4][:, k % 4, :].bitcast(F32)
-            sh = shp.tile([P, 4, P], F32, name="sh")
-            nc.scalar.copy(out=sh[:, 0:2, :], in_=words[:, 512:768].rearrange("p (n u) -> p u n", u=2))
-            nc.scalar.copy(out=sh[:, 2:4, :], in_=vwords.rearrange("p (n u) -> p u n", u=2))
-            st[k]["sh"] = sh
+        def parts(s):
+            return (0 if s + 2 < TILES else 3), (4 if s >= 0 else 3)
 
-        def turn(k):
-            words = mom_t[k][:, k % 2, :].bitcast(F32)
-            vwords = v_t[k // 4][:, k % 4, :].bitcast(F32)
-            bx = ps_tr.tile([P, 4, P], F32, name="bank")
-            for g in range(2):
-                for u in range(2):
-                    nc.tensor.transpose(
-                        bx[:, 2 * g + u, :], words[:, 256 * g + u : 256 * (g + 1) : 2], ident[:]
-                    )
-            by = ps_tr.tile([P, 4, P], F32, name="bank")
-            for u in range(2):
-                nc.tensor.transpose(
-                    by[:, u, :], st[k]["sh"][:, u, :] if "sh" in st[k] else words[:, 512 + u : 768 : 2], ident[:]
-                )
-            for u in range(2):
-                nc.tensor.transpose(
-                    by[:, 2 + u, :], st[k]["sh"][:, 2 + u, :] if "sh" in st[k] else vwords[:, u::2], ident[:]
-                )
-            st[k]["bx"], st[k]["by"] = bx, by
+        def sort_mom(k):
+            srt[k] = small.tile([P, SORTED, 2, P], F32, name="srt")
+            words = mom_t[k].bitcast(F32)[:, 0 : 256 * SORTED]
+            nc.scalar.copy(out=srt[k][:], in_=words.rearrange("p (g n x) -> p g x n", g=SORTED, x=2))
 
-        def empty(k):
-            bx, by = st[k]["bx"], st[k]["by"]
-            mg = work.tile([P, GROUPS, 4 * P], BF16, align_bytes=64, name="mg")
-            mg_words = mg[:].bitcast(F32)
-            nc.scalar.copy(
-                out=mg_words[:, 0:2, :].rearrange("p g (n u) -> p g n u", u=2),
-                in_=bx[:].rearrange("p (g u) n -> p g n u", u=2),
-            )
-            nc.scalar.copy(
-                out=mg_words[:, 2, :].rearrange("p (n u) -> p n u", u=2),
-                in_=by[:, 0:2, :].rearrange("p u n -> p n u"),
-            )
-            rs = rsp.tile([P, P, 2, 2], F32, name="rs")
+        def inv_root(k):
+            rs[k] = rsp.tile([P, 2, P, 2], F32, name="rs")
             nc.scalar.activation(
-                out=rs[:],
-                in_=by[:, 2:4, :].bitcast(BF16).rearrange("p u (n e) -> p n u e", e=2),
+                out=rs[k][:],
+                in_=v_t[k].rearrange("p (m u e) -> p u m e", u=2, e=2),
                 func=ACT.Abs_reciprocal_sqrt,
             )
-            st[k]["mg"], st[k]["rs"] = mg, rs
 
-        def quant_mom(k, parts=(0, 1)):
-            mg = st[k]["mg"]
-            if 0 in parts:
-                st[k]["mc"] = work.tile([P, GROUPS, P], U32, align_bytes=64, name="mc")
-                st[k]["ms"] = work.tile([P, GROUPS, P], U8, align_bytes=64, name="ms")
-            mc, ms = st[k]["mc"], st[k]["ms"]
-            for g0, g1 in [((0, 2), (2, 3))[x] for x in parts]:
-                nc.vector.quantize_mx(
-                    out=mc[:, g0:g1, :].rearrange("p g n -> p (g n)").bitcast(FP8X4),
-                    scales=ms[:, g0:g1, :].rearrange("p g n -> p (g n)"),
-                    in_=mg[:, g0:g1, :].rearrange("p g n -> p (g n)"),
-                )
+        def turn_mom(s):
+            k = s + 2
+            words = mom_t[k].bitcast(F32)
+            bank_x[s] = ps_t.tile([P, 4, P], F32, name="bank")
+            bank_y[s] = ps_t.tile([P, 4, P], F32, name="bank")
+            for g in range(GROUPS):
+                for x in range(2):
+                    dst = bank_x[s][:, 2 * g + x, :] if g < 2 else bank_y[s][:, x, :]
+                    if k in srt and g < SORTED:
+                        src = srt[k][:, g, x, :]
+                    else:
+                        src = words[:, 256 * g + x : 256 * (g + 1) : 2]
+                    nc.tensor.transpose(dst, src, ident[:])
 
-        def project(k, t):
-            mc, ms = st[k]["mc"], st[k]["ms"]
-            if t == 0:
-                st[k]["r"] = ps_r.tile([P, 4, P], F32, name="r")
+        def turn_h(s):
+            if s not in bank_y:
+                bank_y[s] = ps_t.tile([P, 4, P], F32, name="bank")
+            words = h[s][:].bitcast(F32)
+            for x in range(2):
+                nc.tensor.transpose(bank_y[s][:, 2 + x, :], words[:, P * x : P * (x + 1)], ident[:])
+
+        def empty(s):
+            lo, hi = parts(s)
+            q_in[s] = qinp.tile([P, 4, 512], BF16, align_bytes=64, name="q_in")
+            words = q_in[s][:].bitcast(F32).rearrange("p a (n x) -> p a n x", x=2)
+            if lo == 0:
+                nc.scalar.copy(out=words[:, 0:2], in_=bank_x[s][:].rearrange("p (a x) n -> p a n x", x=2))
+            lo = max(lo, 2)
+            nc.scalar.copy(
+                out=words[:, lo:hi],
+                in_=bank_y[s][:].rearrange("p (a x) n -> p a n x", x=2)[:, lo - 2 : hi - 2],
+            )
+
+        def quant(s):
+            lo, hi = parts(s)
+            q_c[s] = qoutp.tile([P, 4, P], U32, align_bytes=64, name="q_c")
+            q_s[s] = qoutp.tile([P, 4, P], U8, align_bytes=64, name="q_s")
+            nc.vector.quantize_mx(
+                out=q_c[s][:, lo:hi, :].rearrange("p a n -> p (a n)").bitcast(FP8X4),
+                scales=q_s[s][:, lo:hi, :].rearrange("p a n -> p (a n)"),
+                in_=q_in[s][:, lo:hi, :].rearrange("p a n -> p (a n)"),
+            )
+
+        def project(k):
+            r_bank[k] = ps_r.tile([P, R], F32, name="r")
             for g in range(GROUPS):
                 nc.tensor.matmul_mx(
-                    out=st[k]["r"][:, t, :],
-                    lhsT=a_c[:, g, P * t : P * (t + 1)].bitcast(FP8X4),
-                    lhsT_scale=a_s[:, g, P * t : P * (t + 1)],
-                    rhs=mc[:, g, :].bitcast(FP8X4),
-                    rhs_scale=ms[:, g, :],
+                    out=r_bank[k][:],
+                    lhsT=q_c[k - 2][:, g, :].bitcast(FP8X4),
+                    lhsT_scale=q_s[k - 2][:, g, :],
+                    rhs=a_c[:, g, :].bitcast(FP8X4),
+                    rhs_scale=a_s[:, g, :],
                     start=(g == 0),
                     stop=(g == GROUPS - 1),
                 )
 
         def direction(k):
-            h = work.tile([P, P, 4], BF16, align_bytes=64, name="h")
+            h[k] = small.tile([P, R], BF16, name="h")
             nc.vector.tensor_tensor(
-                out=h[:],
-                in0=st[k]["r"][:].rearrange("p t n -> p n t"),
-                in1=st[k]["rs"][:].rearrange("p n u e -> p n (u e)"),
+                out=h[k][:],
+                in0=r_bank[k][:],
+                in1=rs[k][:].rearrange("p u m e -> p (u m e)"),
                 op=ALU.mult,
             )
-            st[k]["h"] = h
-
-        def quant_h(k):
-            hc = hqp.tile([P, P], U32, align_bytes=64, name="hc")
-            hs = hqp.tile([P, P], U8, align_bytes=64, name="hs")
-            nc.vector.quantize_mx(
-                out=hc[:].bitcast(FP8X4),
-                scales=hs[:],
-                in_=st[k]["h"][:].rearrange("p n t -> p (n t)"),
-            )
-            st[k]["hc"], st[k]["hs"] = hc, hs
-
-        u_bank = {}
 
         def lift(k, c):
             cols = slice(512 * c, 512 * (c + 1))
-            u = ps_u.tile([P, 4, P], F32, name="u")
+            u_bank[k, c] = ps_u.tile([P, 512], F32, name="u")
             nc.tensor.matmul_mx(
-                out=u[:].rearrange("p a b -> p (a b)"),
-                lhsT=st[k]["hc"][:].bitcast(FP8X4),
-                lhsT_scale=st[k]["hs"][:],
+                out=u_bank[k, c][:],
+                lhsT=q_c[k][:, 3, :].bitcast(FP8X4),
+                lhsT_scale=q_s[k][:, 3, :],
                 rhs=b_c[:, cols].bitcast(FP8X4),
                 rhs_scale=b_s[:, cols],
                 start=True,
                 stop=True,
             )
-            u_bank[k, c] = u
 
         def finish(k, c):
             cols = slice(512 * c, 512 * (c + 1))
-            o = outp.tile([P, 512], F32, name="o")
+            if k not in o_t:
+                o_t[k] = big.tile([P, N], F32, name="o_t", tag="big")
             nc.vector.scalar_tensor_tensor(
-                out=o[:],
-                in0=w_t[k][:, k % 2, cols],
+                out=o_t[k][:, cols],
+                in0=w_t[k][:, cols],
                 scalar=KEEP,
-                in1=u_bank[k, c][:].rearrange("p a b -> p (a b)"),
+                in1=u_bank[k, c][:],
                 op0=ALU.mult,
                 op1=ALU.subtract,
             )
-            nc.sync.dma_start(out=out_v[:, k, cols], in_=o[:])
+            if k >= TILES - 2:
+                nc.sync.dma_start(out=out_v[:, k, cols], in_=o_t[k][:, cols])
+            elif c == CHUNKS - 1:
+                nc.sync.dma_start(out=out_v[:, k, :], in_=o_t[k][:])
 
+        load_v(0, 1)
         for t in range(4):
             load_a(t)
-        load_mom(0, 1)
+        load_mom_single(0)
         load_b(0)
-        load_v(0)
-        load_mom(1, 1)
-        load_mom(2)
         load_b(1)
-        load_w(0)
-        load_b(2)
+        load_mom_single(1)
+        load_v(1, 3)
+        load_mom(2)
         load_mom(4)
-        load_v(1)
-        load_w(2)
-        load_mom(6)
-        load_v(2)
-        load_mom(8)
-        load_w(4)
-        more = [(load_mom, 10), (load_w, 6), (load_v, 3), (load_mom, 12), (load_w, 8), (load_mom, 14), (load_w, 10), (load_w, 12), (load_w, 14)]
+        load_w(0)
+        for j in range(3):
+            load_v(4 + 4 * j, 4)
+            load_mom(6 + 4 * j)
+            load_w(2 + 4 * j)
+            if j < 2:
+                load_mom(8 + 4 * j)
+            load_w(4 + 4 * j)
+        load_w(14)
 
-        V_J, S_J = range(0, 8), range(8, 12)
-        scale_a(0, V_J, "V")
-        scale_a(0, S_J, "S")
-        turn_a(0)
-        scale_a(1, V_J, "V")
-        scale_a(1, S_J, "S")
-        turn_a(1)
-        scale_a(2, V_J, "V")
-        empty_a(0, 0, "S")
-        scale_a(2, S_J, "S")
-        turn_a(2)
-        empty_a(0, 1, "V")
-        scale_a(3, V_J, "V")
-        empty_a(1, 0, "S")
-        scale_a(3, S_J, "S")
-        turn_a(3)
-        turn(0)
+        inv_root(0)
+        for t in range(4):
+            widen_a(t)
+            if t == 2:
+                turn_mom(-2)
+            turn_a(t)
+        for g in range(GROUPS):
+            empty_a(g, 0, "S")
+        empty(-2)
+        for t in range(4):
+            widen_b(t, "V")
+        quant(-2)
+        empty_a(0, 1, "S")
         empty_a(1, 1, "V")
-        empty_a(2, 1, "V")
-        empty_a(2, 0, "S")
-        empty_a(3, 0, "V")
-        empty_a(3, 1, "V")
-        empty(0)
-        turn(1)
-        empty(1)
+        empty_a(2, 1, "S")
+        turn_mom(-1)
         quant_a(0)
         quant_a(1)
         quant_a(2)
-
-        queue, outstanding = [], []
-        allowed = {0}
-
-        def next_final():
-            for x in queue:
-                if x[1] in allowed:
-                    queue.remove(x)
-                    return x
-            return None
-
-        def step(s, n, ev=(), es=(), sh=False):
-            ev, es = list(ev), list(es)
-            if sh and s + 4 < TILES:
-                shuffle(s + 4)
-            if s + 3 < TILES:
-                turn(s + 3)
-            vec = [lambda: direction(s), lambda: quant_mom(s + 2), lambda: quant_h(s), lambda: None]
-            on = [s < TILES, s + 2 < TILES, s < TILES, False]
-            for i in range(4):
-                if outstanding and (i < 3 or n > 3):
-                    finish(*outstanding.pop(0))
-                if s + 1 < TILES:
-                    project(s + 1, i)
-                if i < n:
-                    x = next_final()
-                    if x is not None:
-                        lift(*x)
-                        outstanding.append(x)
-                if on[i]:
-                    vec[i]()
-                if ev:
-                    ev.pop(0)()
-            for f in ev:
-                f()
-            if s + 3 < TILES:
-                empty(s + 3)
-            for f in es:
-                f()
-            if s < TILES:
-                queue.extend((s, c) for c in range(CHUNKS))
-            if more:
-                f, a = more.pop(0)
-                f(a)
-        quant_mom(0)
-        widen_b(0, 0, 4, "V")
-        for t in range(4):
-            project(0, t)
-        turn(2)
-        scale_b(0, (0, 1, 2, 3), "V")
-        quant_mom(1)
+        empty(-1)
+        inv_root(1)
+        project(0)
+        turn_mom(0)
+        scale_b(0, range(0, 2), "V")
+        quant(-1)
+        direction(0)
+        turn_h(0)
+        project(1)
+        scale_b(1, range(0, 2), "S")
+        empty(0)
+        scale_b(0, range(2, 4), "V")
         quant_b(0)
-        empty(2)
+        turn_mom(1)
+        scale_b(1, range(2, 4), "S")
 
-        step(0, 0, (lambda: widen_b(1, 0, 4, "V"), lambda: scale_b(1, (0, 1), "V")), (lambda: scale_b(1, (2, 3), "S"),))
-        step(1, 1, (lambda: quant_b(1),), (lambda: widen_b(2, 0, 4, "S"),))
-        allowed.add(1)
-        step(2, 2, (lambda: scale_b(2, (0, 1), "V"),), (lambda: scale_b(2, (2, 3), "S"),))
-        step(3, 3, (lambda: quant_b(2),))
-        allowed.add(2)
-        for s in range(4, TILES):
-            step(s, 4 if len(queue) > 4 else 3, sh=True)
-        while queue or outstanding:
-            step(TILES, 3)
+        for s in range(TILES + 1):
+            if s < TILES:
+                quant(s)
+            if s == 0:
+                direction(1)
+                turn_h(1)
+                empty(1)
+                inv_root(2)
+                inv_root(3)
+                scale_b(2, range(4), "V")
+                quant_b(1)
+                quant_b(2)
+            if s + 2 < TILES:
+                project(s + 2)
+            for c in range(CHUNKS):
+                if s >= 1:
+                    finish(s - 1, c)
+                if s < TILES:
+                    lift(s, c)
+            if s + 2 < TILES:
+                direction(s + 2)
+            if s + 4 < TILES:
+                turn_mom(s + 2)
+            if s + 2 < TILES:
+                turn_h(s + 2)
+                empty(s + 2)
+            if s + 5 < TILES:
+                sort_mom(s + 5)
+            if s + 4 < TILES:
+                inv_root(s + 4)

@@ -23,6 +23,7 @@ GROUPS = N // 512
 NBLK = N // P
 CHUNKS = N // 512
 SORTED = 2
+PAIRED = 8
 A_ON_VECTOR = 8
 
 
@@ -39,7 +40,7 @@ def tile_lowrank_adam_style_step_d7_kernel(
 
     with ExitStack() as ctx:
         keep = ctx.enter_context(tc.tile_pool(name="keep", bufs=1))
-        big = ctx.enter_context(tc.tile_pool(name="big", bufs=19))
+        big = ctx.enter_context(tc.tile_pool(name="big", bufs=9))
         groupp = ctx.enter_context(tc.tile_pool(name="groupp", bufs=4))
         qinp = ctx.enter_context(tc.tile_pool(name="qinp", bufs=3))
         qoutp = ctx.enter_context(tc.tile_pool(name="qoutp", bufs=3))
@@ -65,7 +66,7 @@ def tile_lowrank_adam_style_step_d7_kernel(
         ident = keep.tile([P, P], F32)
         make_identity(nc, ident[:])
 
-        mom_t, v_t, w_t, o_t = {}, {}, {}, {}
+        mom_t, v_t, w_t, o_t, o_pair = {}, {}, {}, {}, {}
         a_b = [keep.tile([P, N], U8, name="a_b%d" % t) for t in range(4)]
         b_b = [keep.tile([P, 2, N], U8, name="b_b%d" % x) for x in range(2)]
 
@@ -76,14 +77,16 @@ def tile_lowrank_adam_style_step_d7_kernel(
             nc.sync.dma_start(out=b_b[x][:], in_=b_rows[:, 2 * x : 2 * x + 2, :])
 
         def load_mom(k):
-            pair = big.tile([P, 2, N], BF16, name="mom_pair", tag="big")
-            nc.sync.dma_start(out=pair[:], in_=mom_v[:, k : k + 2, :])
-            mom_t[k], mom_t[k + 1] = pair[:, 0, :], pair[:, 1, :]
+            four = big.tile([P, 4, N], BF16, name="mom_four", tag="big")
+            nc.sync.dma_start(out=four[:], in_=mom_v[:, k : k + 4, :])
+            for i in range(4):
+                mom_t[k + i] = four[:, i, :]
 
-        def load_mom_single(k):
-            one = keep.tile([P, N], BF16, name="mom_one%d" % k)
-            nc.sync.dma_start(out=one[:], in_=mom_v[:, k, :])
-            mom_t[k] = one[:]
+        def load_mom_early(k, n):
+            few = keep.tile([P, n, N], BF16, name="mom_early%d" % k)
+            nc.sync.dma_start(out=few[:], in_=mom_v[:, k : k + n, :])
+            for i in range(n):
+                mom_t[k + i] = few[:, i, :]
 
         def load_v(k, n):
             vt = keep.tile([P, n, R], BF16, name="v_t%d" % k)
@@ -92,9 +95,10 @@ def tile_lowrank_adam_style_step_d7_kernel(
                 v_t[k + i] = vt[:, i, :]
 
         def load_w(k):
-            pair = big.tile([P, 2, N], BF16, name="w_pair", tag="big")
-            nc.sync.dma_start(out=pair[:], in_=w_v[:, k : k + 2, :])
-            w_t[k], w_t[k + 1] = pair[:, 0, :], pair[:, 1, :]
+            four = big.tile([P, 4, N], BF16, name="w_four", tag="big")
+            nc.sync.dma_start(out=four[:], in_=w_v[:, k : k + 4, :])
+            for i in range(4):
+                w_t[k + i] = four[:, i, :]
 
         def move(eng, dst, src):
             if eng == "S":
@@ -275,8 +279,9 @@ def tile_lowrank_adam_style_step_d7_kernel(
 
         def finish(k, c):
             cols = slice(512 * c, 512 * (c + 1))
-            if k not in o_t:
-                o_t[k] = big.tile([P, N], F32, name="o_t", tag="big")
+            if k % 2 == 0 and c == 0:
+                o_pair[k] = big.tile([P, 2, N], F32, name="o_pair", tag="big")
+                o_t[k], o_t[k + 1] = o_pair[k][:, 0, :], o_pair[k][:, 1, :]
             nc.vector.scalar_tensor_tensor(
                 out=o_t[k][:, cols],
                 in0=w_t[k][:, cols],
@@ -287,28 +292,27 @@ def tile_lowrank_adam_style_step_d7_kernel(
             )
             if k >= TILES - 2:
                 nc.sync.dma_start(out=out_v[:, k, cols], in_=o_t[k][:, cols])
-            elif c == CHUNKS - 1:
-                nc.sync.dma_start(out=out_v[:, k, :], in_=o_t[k][:])
+            elif c == CHUNKS - 1 and k >= PAIRED:
+                nc.sync.dma_start(out=out_v[:, k, :], in_=o_t[k])
+            elif c == CHUNKS - 1 and k % 2 == 1:
+                nc.sync.dma_start(out=out_v[:, k - 1 : k + 1, :], in_=o_pair[k - 1][:])
 
         load_v(0, 1)
         for t in range(4):
             load_a(t)
-        load_mom_single(0)
+        load_mom_early(0, 1)
         load_b(0)
         load_b(1)
-        load_mom_single(1)
+        load_mom_early(1, 1)
         load_v(1, 3)
-        load_mom(2)
+        load_mom_early(2, 2)
         load_mom(4)
         load_w(0)
-        for j in range(3):
-            load_v(4 + 4 * j, 4)
-            load_mom(6 + 4 * j)
-            load_w(2 + 4 * j)
-            if j < 2:
-                load_mom(8 + 4 * j)
-            load_w(4 + 4 * j)
-        load_w(14)
+        load_v(4, 12)
+        for k in (8, 12):
+            load_mom(k)
+            load_w(k - 4)
+        load_w(12)
 
         inv_root(0)
         for t in range(4):

@@ -24,6 +24,8 @@ NBLK = N // P
 CHUNKS = N // 512
 SORTED = 2
 PAIRED = 8
+CHUNKED = 11
+AHEAD = 3
 A_ON_VECTOR = 8
 
 
@@ -184,7 +186,7 @@ def tile_lowrank_adam_style_step_d7_kernel(
         bank_x, bank_y, q_in, q_c, q_s = {}, {}, {}, {}, {}
 
         def parts(s):
-            return (0 if s + 2 < TILES else 3), (4 if s >= 0 else 3)
+            return (0 if s + AHEAD < TILES else 3), (4 if s >= 0 else 3)
 
         def sort_mom(k):
             srt[k] = small.tile([P, SORTED, 2, P], F32, name="srt")
@@ -200,7 +202,7 @@ def tile_lowrank_adam_style_step_d7_kernel(
             )
 
         def turn_mom(s):
-            k = s + 2
+            k = s + AHEAD
             words = mom_t[k].bitcast(F32)
             bank_x[s] = ps_t.tile([P, 4, P], F32, name="bank")
             bank_y[s] = ps_t.tile([P, 4, P], F32, name="bank")
@@ -247,8 +249,8 @@ def tile_lowrank_adam_style_step_d7_kernel(
             for g in range(GROUPS):
                 nc.tensor.matmul_mx(
                     out=r_bank[k][:],
-                    lhsT=q_c[k - 2][:, g, :].bitcast(FP8X4),
-                    lhsT_scale=q_s[k - 2][:, g, :],
+                    lhsT=q_c[k - AHEAD][:, g, :].bitcast(FP8X4),
+                    lhsT_scale=q_s[k - AHEAD][:, g, :],
                     rhs=a_c[:, g, :].bitcast(FP8X4),
                     rhs_scale=a_s[:, g, :],
                     start=(g == 0),
@@ -290,7 +292,7 @@ def tile_lowrank_adam_style_step_d7_kernel(
                 op0=ALU.mult,
                 op1=ALU.subtract,
             )
-            if k >= TILES - 2:
+            if k >= CHUNKED:
                 nc.sync.dma_start(out=out_v[:, k, cols], in_=o_t[k][:, cols])
             elif c == CHUNKS - 1 and k >= PAIRED:
                 nc.sync.dma_start(out=out_v[:, k, :], in_=o_t[k])
@@ -318,51 +320,55 @@ def tile_lowrank_adam_style_step_d7_kernel(
         for t in range(4):
             widen_a(t)
             if t == 2:
-                turn_mom(-2)
+                turn_mom(-3)
             turn_a(t)
         for g in range(GROUPS):
             empty_a(g, 0, "S")
-        empty(-2)
+        empty(-3)
         for t in range(4):
             widen_b(t, "V")
-        quant(-2)
+        quant(-3)
         empty_a(0, 1, "S")
         empty_a(1, 1, "V")
         empty_a(2, 1, "S")
-        turn_mom(-1)
+        turn_mom(-2)
         quant_a(0)
         quant_a(1)
         quant_a(2)
-        empty(-1)
+        empty(-2)
         inv_root(1)
-        project(0)
-        turn_mom(0)
-        scale_b(0, range(0, 2), "V")
-        quant(-1)
-        direction(0)
-        turn_h(0)
-        project(1)
         scale_b(1, range(0, 2), "S")
-        empty(0)
-        scale_b(0, range(2, 4), "V")
-        quant_b(0)
-        turn_mom(1)
+        project(0)
+        turn_mom(-1)
+        scale_b(0, range(0, 2), "V")
+        quant(-2)
+        direction(0)
+        empty(-1)
         scale_b(1, range(2, 4), "S")
+        project(1)
+        turn_mom(0)
+        turn_h(0)
+        scale_b(0, range(2, 4), "V")
+        quant(-1)
+        project(2)
+        empty(0)
+        quant_b(0)
+        direction(1)
+        inv_root(2)
+        turn_mom(1)
+        turn_h(1)
+        empty(1)
+        scale_b(2, range(4), "V")
+        inv_root(3)
 
         for s in range(TILES + 1):
+            if s >= 1 and s + 2 < TILES:
+                project(s + 2)
             if s < TILES:
                 quant(s)
             if s == 0:
-                direction(1)
-                turn_h(1)
-                empty(1)
-                inv_root(2)
-                inv_root(3)
-                scale_b(2, range(4), "V")
                 quant_b(1)
                 quant_b(2)
-            if s + 2 < TILES:
-                project(s + 2)
             for c in range(CHUNKS):
                 if s >= 1:
                     finish(s - 1, c)
@@ -370,12 +376,12 @@ def tile_lowrank_adam_style_step_d7_kernel(
                     lift(s, c)
             if s + 2 < TILES:
                 direction(s + 2)
+            if s + 3 + AHEAD < TILES:
+                sort_mom(s + 3 + AHEAD)
             if s + 4 < TILES:
+                inv_root(s + 4)
+            if s + 2 + AHEAD < TILES:
                 turn_mom(s + 2)
             if s + 2 < TILES:
                 turn_h(s + 2)
                 empty(s + 2)
-            if s + 5 < TILES:
-                sort_mom(s + 5)
-            if s + 4 < TILES:
-                inv_root(s + 4)

@@ -68,6 +68,16 @@ def tile_lowrank_adam_style_step_d7_kernel(
         ident = keep.tile([P, P], F32)
         make_identity(nc, ident[:])
 
+        def warm_up(pool, name, blocks):
+            idle = pool.tile([P, 4, P], F32, name=name)
+            nc.tensor.matmul(
+                idle[:, 0:blocks, :],
+                lhsT=ident[:],
+                rhs=ident[:].unsqueeze(1).to_broadcast([P, blocks, P]),
+                start=True,
+                stop=True,
+            )
+
         mom_t, v_t, w_t, o_t, o_pair = {}, {}, {}, {}, {}
         a_b = [keep.tile([P, N], U8, name="a_b%d" % t) for t in range(4)]
         b_b = [keep.tile([P, 2, N], U8, name="b_b%d" % x) for x in range(2)]
@@ -159,8 +169,8 @@ def tile_lowrank_adam_style_step_d7_kernel(
         b_s = keep.tile([P, N], U8, align_bytes=64)
         b_g = {}
 
-        def widen_b(t, eng):
-            move(eng, b_wide[:, t, :], b_b[t // 2][:, t % 2, :].bitcast(FP8))
+        def widen_b(t, eng, cols=slice(0, N)):
+            move(eng, b_wide[:, t, cols], b_b[t // 2][:, t % 2, cols].bitcast(FP8))
 
         def scale_b(c, js, eng):
             if c not in b_g:
@@ -317,56 +327,68 @@ def tile_lowrank_adam_style_step_d7_kernel(
         load_w(12)
 
         inv_root(0)
+        warm_up(ps_r, "r", 4)
+        warm_up(ps_r, "r", 2)
         for t in range(4):
             widen_a(t)
-            if t == 2:
-                turn_mom(-3)
-            turn_a(t)
+        turn_a(0)
+        warm_up(ps_r, "r", 2)
+        turn_a(1)
         for g in range(GROUPS):
             empty_a(g, 0, "S")
+        turn_mom(-3)
+        warm_up(ps_r, "r", 3)
+        turn_a(2)
+        turn_a(3)
         empty(-3)
-        for t in range(4):
+        for t in range(3):
             widen_b(t, "V")
+        widen_b(3, "S", slice(0, N // 2))
         quant(-3)
         empty_a(0, 1, "S")
         empty_a(1, 1, "V")
         empty_a(2, 1, "S")
+        warm_up(ps_u, "u", 3)
         turn_mom(-2)
         quant_a(0)
         quant_a(1)
         quant_a(2)
+        widen_b(3, "S", slice(N // 2, N))
         empty(-2)
         inv_root(1)
-        scale_b(1, range(0, 2), "S")
         project(0)
         turn_mom(-1)
-        scale_b(0, range(0, 2), "V")
+        scale_b(0, range(0, 1), "V")
         quant(-2)
         direction(0)
+        scale_b(2, range(0, 1), "S")
         empty(-1)
-        scale_b(1, range(2, 4), "S")
         project(1)
         turn_mom(0)
         turn_h(0)
-        scale_b(0, range(2, 4), "V")
+        scale_b(0, range(1, 4), "V")
         quant(-1)
         project(2)
+        scale_b(2, range(1, 2), "S")
         empty(0)
-        quant_b(0)
         direction(1)
+        quant_b(0)
         inv_root(2)
         turn_mom(1)
         turn_h(1)
+        scale_b(2, range(2, 3), "S")
         empty(1)
-        scale_b(2, range(4), "V")
+        scale_b(2, range(3, 4), "S")
         inv_root(3)
 
         for s in range(TILES + 1):
-            if s >= 1 and s + 2 < TILES:
-                project(s + 2)
             if s < TILES:
                 quant(s)
+            if s + AHEAD < TILES:
+                project(s + AHEAD)
             if s == 0:
+                scale_b(1, range(4), "V")
+                direction(2)
                 quant_b(1)
                 quant_b(2)
             for c in range(CHUNKS):
@@ -374,7 +396,7 @@ def tile_lowrank_adam_style_step_d7_kernel(
                     finish(s - 1, c)
                 if s < TILES:
                     lift(s, c)
-            if s + 2 < TILES:
+            if s >= 1 and s + 2 < TILES:
                 direction(s + 2)
             if s + 3 + AHEAD < TILES:
                 sort_mom(s + 3 + AHEAD)

@@ -26,6 +26,7 @@ SORTED = 2
 PAIRED = 8
 CHUNKED = 11
 AHEAD = 3
+Q_SLOTS = 3
 A_ON_VECTOR = 8
 
 
@@ -44,7 +45,7 @@ def tile_lowrank_adam_style_step_d7_kernel(
         keep = ctx.enter_context(tc.tile_pool(name="keep", bufs=1))
         big = ctx.enter_context(tc.tile_pool(name="big", bufs=9))
         groupp = ctx.enter_context(tc.tile_pool(name="groupp", bufs=4))
-        qinp = ctx.enter_context(tc.tile_pool(name="qinp", bufs=3))
+        qinp = ctx.enter_context(tc.tile_pool(name="qinp", bufs=1))
         qoutp = ctx.enter_context(tc.tile_pool(name="qoutp", bufs=3))
         small = ctx.enter_context(tc.tile_pool(name="small", bufs=2))
         rsp = ctx.enter_context(tc.tile_pool(name="rsp", bufs=3))
@@ -67,16 +68,6 @@ def tile_lowrank_adam_style_step_d7_kernel(
         b_sc = sc_all[:, 16 : 16 + NBLK]
         ident = keep.tile([P, P], F32)
         make_identity(nc, ident[:])
-
-        def warm_up(pool, name, blocks):
-            idle = pool.tile([P, 4, P], F32, name=name)
-            nc.tensor.matmul(
-                idle[:, 0:blocks, :],
-                lhsT=ident[:],
-                rhs=ident[:].unsqueeze(1).to_broadcast([P, blocks, P]),
-                start=True,
-                stop=True,
-            )
 
         mom_t, v_t, w_t, o_t, o_pair = {}, {}, {}, {}, {}
         a_b = [keep.tile([P, N], U8, name="a_b%d" % t) for t in range(4)]
@@ -192,7 +183,7 @@ def tile_lowrank_adam_style_step_d7_kernel(
                 in_=b_g[c][:].rearrange("p n t -> p (n t)"),
             )
 
-        srt, rs, h, r_bank, u_bank = {}, {}, {}, {}, {}
+        srt, rs, h, r_bank, r_sb, u_bank = {}, {}, {}, {}, {}, {}
         bank_x, bank_y, q_in, q_c, q_s = {}, {}, {}, {}, {}
 
         def parts(s):
@@ -234,7 +225,10 @@ def tile_lowrank_adam_style_step_d7_kernel(
 
         def empty(s):
             lo, hi = parts(s)
-            q_in[s] = qinp.tile([P, 4, 512], BF16, align_bytes=64, name="q_in")
+            slot = s % Q_SLOTS
+            q_in[s] = qinp.tile(
+                [P, 4, 512], BF16, align_bytes=64, name="q_in%d" % slot, offset=4096 * slot
+            )
             words = q_in[s][:].bitcast(F32).rearrange("p a (n x) -> p a n x", x=2)
             if lo == 0:
                 nc.scalar.copy(out=words[:, 0:2], in_=bank_x[s][:].rearrange("p (a x) n -> p a n x", x=2))
@@ -272,6 +266,20 @@ def tile_lowrank_adam_style_step_d7_kernel(
             nc.vector.tensor_tensor(
                 out=h[k][:],
                 in0=r_bank[k][:],
+                in1=rs[k][:].rearrange("p u m e -> p (u m e)"),
+                op=ALU.mult,
+            )
+
+        def fetch_r(k):
+            r_sb[k] = keep.tile([P, R], F32, name="r_sb")
+            nc.scalar.copy(out=r_sb[k][:], in_=r_bank[k][:])
+
+        def direction_gpsimd(k):
+            slot = (k - 2) % Q_SLOTS
+            h[k] = qinp.tile([P, R], BF16, align_bytes=64, name="h%d" % slot, offset=4096 * slot + 3072)
+            nc.gpsimd.tensor_tensor(
+                out=h[k][:],
+                in0=r_sb[k][:],
                 in1=rs[k][:].rearrange("p u m e -> p (u m e)"),
                 op=ALU.mult,
             )
@@ -327,17 +335,13 @@ def tile_lowrank_adam_style_step_d7_kernel(
         load_w(12)
 
         inv_root(0)
-        warm_up(ps_r, "r", 4)
-        warm_up(ps_r, "r", 2)
         for t in range(4):
             widen_a(t)
         turn_a(0)
-        warm_up(ps_r, "r", 2)
         turn_a(1)
         for g in range(GROUPS):
             empty_a(g, 0, "S")
         turn_mom(-3)
-        warm_up(ps_r, "r", 3)
         turn_a(2)
         turn_a(3)
         empty(-3)
@@ -348,7 +352,6 @@ def tile_lowrank_adam_style_step_d7_kernel(
         empty_a(0, 1, "S")
         empty_a(1, 1, "V")
         empty_a(2, 1, "S")
-        warm_up(ps_u, "u", 3)
         turn_mom(-2)
         quant_a(0)
         quant_a(1)
@@ -391,17 +394,21 @@ def tile_lowrank_adam_style_step_d7_kernel(
                 direction(2)
                 quant_b(1)
                 quant_b(2)
+            if s % 2 == 1 and s + 2 < TILES:
+                direction_gpsimd(s + 2)
             for c in range(CHUNKS):
                 if s >= 1:
                     finish(s - 1, c)
                 if s < TILES:
                     lift(s, c)
-            if s >= 1 and s + 2 < TILES:
-                direction(s + 2)
+            if s % 2 == 1 and s + 3 < TILES:
+                direction(s + 3)
             if s + 3 + AHEAD < TILES:
                 sort_mom(s + 3 + AHEAD)
             if s + 4 < TILES:
                 inv_root(s + 4)
+            if s % 2 == 0 and s + 3 < TILES:
+                fetch_r(s + 3)
             if s + 2 + AHEAD < TILES:
                 turn_mom(s + 2)
             if s + 2 < TILES:

@@ -24,7 +24,7 @@ NBLK = N // P
 CHUNKS = N // 512
 SORTED = 2
 PAIRED = 8
-CHUNKED = 11
+CHUNKED = 12
 AHEAD = 3
 Q_SLOTS = 3
 A_ON_VECTOR = 8
@@ -384,31 +384,56 @@ def tile_lowrank_adam_style_step_d7_kernel(
         scale_b(2, range(3, 4), "S")
         inv_root(3)
 
-        for s in range(TILES + 1):
+        def on_gpsimd(k):
+            return 4 <= k < TILES and (k % 2 == 0 or k + AHEAD >= TILES)
+
+        quant(0)
+        project(3)
+        lift(0, 0)
+        direction(2)
+        turn_mom(2)
+        turn_h(2)
+        empty(2)
+        sort_mom(6)
+        inv_root(4)
+        scale_b(1, range(4), "V")
+        quant(1)
+        project(4)
+        quant_b(1)
+        lift(0, 1)
+        quant_b(2)
+        lift(0, 2)
+        for c in range(CHUNKS):
+            finish(0, c)
+            lift(1, c)
+            if c == 0:
+                direction(3)
+        turn_mom(3)
+        turn_h(3)
+        sort_mom(7)
+        fetch_r(4)
+        inv_root(5)
+        empty(3)
+
+        for s in range(2, TILES + 1):
             if s < TILES:
                 quant(s)
             if s + AHEAD < TILES:
                 project(s + AHEAD)
-            if s == 0:
-                scale_b(1, range(4), "V")
-                direction(2)
-                quant_b(1)
-                quant_b(2)
-            if s % 2 == 1 and s + 2 < TILES:
+            if on_gpsimd(s + 2):
                 direction_gpsimd(s + 2)
             for c in range(CHUNKS):
-                if s >= 1:
-                    finish(s - 1, c)
+                finish(s - 1, c)
                 if s < TILES:
                     lift(s, c)
-            if s % 2 == 1 and s + 3 < TILES:
-                direction(s + 3)
+            if s + 2 < TILES and not on_gpsimd(s + 2):
+                direction(s + 2)
             if s + 3 + AHEAD < TILES:
                 sort_mom(s + 3 + AHEAD)
+            if on_gpsimd(s + 3):
+                fetch_r(s + 3)
             if s + 4 < TILES:
                 inv_root(s + 4)
-            if s % 2 == 0 and s + 3 < TILES:
-                fetch_r(s + 3)
             if s + 2 + AHEAD < TILES:
                 turn_mom(s + 2)
             if s + 2 < TILES:

@@ -23,10 +23,11 @@ GROUPS = N // 512
 NBLK = N // P
 CHUNKS = N // 512
 SORTED = 2
-PAIRED = 8
-CHUNKED = 12
+PAIRED = 10
+CHUNKED = 13
 AHEAD = 3
 Q_SLOTS = 3
+DMA_ALIGN = 256
 A_ON_VECTOR = 8
 
 
@@ -70,8 +71,8 @@ def tile_lowrank_adam_style_step_d7_kernel(
         make_identity(nc, ident[:])
 
         mom_t, v_t, w_t, o_t, o_pair = {}, {}, {}, {}, {}
-        a_b = [keep.tile([P, N], U8, name="a_b%d" % t) for t in range(4)]
-        b_b = [keep.tile([P, 2, N], U8, name="b_b%d" % x) for x in range(2)]
+        a_b = [keep.tile([P, N], U8, align_bytes=DMA_ALIGN, name="a_b%d" % t) for t in range(4)]
+        b_b = [keep.tile([P, 2, N], U8, align_bytes=DMA_ALIGN, name="b_b%d" % x) for x in range(2)]
 
         def load_a(t):
             nc.sync.dma_start(out=a_b[t][:], in_=a_rows[:, t, :])
@@ -80,25 +81,25 @@ def tile_lowrank_adam_style_step_d7_kernel(
             nc.sync.dma_start(out=b_b[x][:], in_=b_rows[:, 2 * x : 2 * x + 2, :])
 
         def load_mom(k):
-            four = big.tile([P, 4, N], BF16, name="mom_four", tag="big")
+            four = big.tile([P, 4, N], BF16, align_bytes=DMA_ALIGN, name="mom_four", tag="big")
             nc.sync.dma_start(out=four[:], in_=mom_v[:, k : k + 4, :])
             for i in range(4):
                 mom_t[k + i] = four[:, i, :]
 
         def load_mom_early(k, n):
-            few = keep.tile([P, n, N], BF16, name="mom_early%d" % k)
+            few = keep.tile([P, n, N], BF16, align_bytes=DMA_ALIGN, name="mom_early%d" % k)
             nc.sync.dma_start(out=few[:], in_=mom_v[:, k : k + n, :])
             for i in range(n):
                 mom_t[k + i] = few[:, i, :]
 
         def load_v(k, n):
-            vt = keep.tile([P, n, R], BF16, name="v_t%d" % k)
+            vt = keep.tile([P, n, R], BF16, align_bytes=DMA_ALIGN, name="v_t%d" % k)
             nc.sync.dma_start(out=vt[:], in_=v_v[:, k : k + n, :])
             for i in range(n):
                 v_t[k + i] = vt[:, i, :]
 
         def load_w(k):
-            four = big.tile([P, 4, N], BF16, name="w_four", tag="big")
+            four = big.tile([P, 4, N], BF16, align_bytes=DMA_ALIGN, name="w_four", tag="big")
             nc.sync.dma_start(out=four[:], in_=w_v[:, k : k + 4, :])
             for i in range(4):
                 w_t[k + i] = four[:, i, :]
@@ -115,7 +116,7 @@ def tile_lowrank_adam_style_step_d7_kernel(
             else:
                 nc.vector.tensor_scalar(out=dst, in0=src, scalar1=sc, scalar2=None, op0=ALU.mult)
 
-        a_wide = [keep.tile([P, N], BF16, name="a_wide%d" % t) for t in range(4)]
+        a_wide = [keep.tile([P, N], BF16, name="a_wide%d" % t, tag="a_wide%d" % t) for t in range(4)]
         a_c = keep.tile([P, GROUPS, R], U32, align_bytes=64)
         a_s = keep.tile([P, GROUPS, R], U8, align_bytes=64)
         a_g, a_bank = {}, {}
@@ -271,7 +272,7 @@ def tile_lowrank_adam_style_step_d7_kernel(
             )
 
         def fetch_r(k):
-            r_sb[k] = keep.tile([P, R], F32, name="r_sb")
+            r_sb[k] = keep.tile([P, R], F32, name="r_sb", tag="a_wide0")
             nc.scalar.copy(out=r_sb[k][:], in_=r_bank[k][:])
 
         def direction_gpsimd(k):
@@ -300,7 +301,7 @@ def tile_lowrank_adam_style_step_d7_kernel(
         def finish(k, c):
             cols = slice(512 * c, 512 * (c + 1))
             if k % 2 == 0 and c == 0:
-                o_pair[k] = big.tile([P, 2, N], F32, name="o_pair", tag="big")
+                o_pair[k] = big.tile([P, 2, N], F32, align_bytes=DMA_ALIGN, name="o_pair", tag="big")
                 o_t[k], o_t[k + 1] = o_pair[k][:, 0, :], o_pair[k][:, 1, :]
             nc.vector.scalar_tensor_tensor(
                 out=o_t[k][:, cols],

@@ -132,12 +132,10 @@ def tile_lowrank_adam_style_step_d7_kernel(
             words = a_wide[t][:].bitcast(F32)
             for g in range(GROUPS):
                 if e == 0:
-                    if u == 0:
-                        a_bank[g, u] = ps_u.tile([P, 4, P], F32, name="u")
-                    elif g < 2:
+                    if u == 1 and g < 2:
                         a_bank[g, u] = ps_r.tile([P, 4, P], F32, name="r")
                     else:
-                        a_bank[g, u] = ps_t.tile([P, 4, P], F32, name="bank")
+                        a_bank[g, u] = ps_u.tile([P, 4, P], F32, name="u")
                 for x in range(2):
                     nc.tensor.transpose(
                         a_bank[g, u][:, 2 * e + x, :], words[:, 256 * g + x : 256 * (g + 1) : 2], ident[:]
@@ -321,18 +319,20 @@ def tile_lowrank_adam_style_step_d7_kernel(
         load_v(0, 1)
         for t in range(4):
             load_a(t)
-        load_mom_early(0, 1)
         load_b(0)
+        load_mom_early(0, 1)
         load_b(1)
         load_mom_early(1, 1)
         load_v(1, 3)
         load_mom_early(2, 2)
         load_mom(4)
+        load_v(4, 4)
         load_w(0)
-        load_v(4, 12)
-        for k in (8, 12):
-            load_mom(k)
-            load_w(k - 4)
+        load_mom(8)
+        load_v(8, 8)
+        load_w(4)
+        load_mom(12)
+        load_w(8)
         load_w(12)
 
         inv_root(0)
@@ -342,41 +342,41 @@ def tile_lowrank_adam_style_step_d7_kernel(
         turn_a(1)
         for g in range(GROUPS):
             empty_a(g, 0, "S")
-        turn_mom(-3)
         turn_a(2)
+        turn_mom(-3)
         turn_a(3)
         empty(-3)
         for t in range(3):
             widen_b(t, "V")
-        widen_b(3, "S", slice(0, N // 2))
-        quant(-3)
-        empty_a(0, 1, "S")
-        empty_a(1, 1, "V")
+        empty_a(0, 1, "V")
+        empty_a(1, 1, "S")
         empty_a(2, 1, "S")
+        quant(-3)
         turn_mom(-2)
         quant_a(0)
         quant_a(1)
         quant_a(2)
-        widen_b(3, "S", slice(N // 2, N))
         empty(-2)
-        inv_root(1)
+        widen_b(3, "S")
         project(0)
         turn_mom(-1)
-        scale_b(0, range(0, 1), "V")
         quant(-2)
+        scale_b(0, range(0, 2), "V")
         direction(0)
+        inv_root(1)
         scale_b(2, range(0, 1), "S")
         empty(-1)
         project(1)
         turn_mom(0)
         turn_h(0)
-        scale_b(0, range(1, 4), "V")
+        scale_b(0, range(2, 4), "V")
         quant(-1)
         project(2)
         scale_b(2, range(1, 2), "S")
         empty(0)
         direction(1)
         quant_b(0)
+        scale_b(1, range(0, 2), "V")
         inv_root(2)
         turn_mom(1)
         turn_h(1)
@@ -397,7 +397,7 @@ def tile_lowrank_adam_style_step_d7_kernel(
         empty(2)
         sort_mom(6)
         inv_root(4)
-        scale_b(1, range(4), "V")
+        scale_b(1, range(2, 4), "V")
         quant(1)
         project(4)
         quant_b(1)
@@ -417,6 +417,9 @@ def tile_lowrank_adam_style_step_d7_kernel(
         empty(3)
 
         for s in range(2, TILES + 1):
+            late = s + AHEAD > TILES
+            if late:
+                finish(s - 1, 0)
             if s < TILES:
                 quant(s)
             if s + AHEAD < TILES:
@@ -424,7 +427,8 @@ def tile_lowrank_adam_style_step_d7_kernel(
             if on_gpsimd(s + 2):
                 direction_gpsimd(s + 2)
             for c in range(CHUNKS):
-                finish(s - 1, c)
+                if c > 0 or not late:
+                    finish(s - 1, c)
                 if s < TILES:
                     lift(s, c)
             if s + 2 < TILES and not on_gpsimd(s + 2):

@@ -22,13 +22,16 @@ TILES = M // P
 GROUPS = N // 512
 NBLK = N // P
 CHUNKS = N // 512
-SORTED = 2
-PAIRED = 10
-CHUNKED = 13
 AHEAD = 3
 Q_SLOTS = 3
 DMA_ALIGN = 256
 A_ON_VECTOR = 8
+KIB = 1024
+MOM_AT, W_AT, V_AT = 0, 48 * KIB, 96 * KIB
+A_AT, B_AT, BG_AT = 112 * KIB, 136 * KIB, 160 * KIB
+OUT_AT = {0: A_AT, 4: B_AT, 7: MOM_AT, 11: MOM_AT + 24 * KIB}
+STORES = (0, 4, 7, 9, 10, 11, 12, 13)
+PIECES = {13: ((0, 2), (2, 3)), 14: ((0, 2), (2, 3)), 15: ((0, 1), (1, 2), (2, 3))}
 
 
 def tile_lowrank_adam_style_step_d7_kernel(
@@ -44,8 +47,7 @@ def tile_lowrank_adam_style_step_d7_kernel(
 
     with ExitStack() as ctx:
         keep = ctx.enter_context(tc.tile_pool(name="keep", bufs=1))
-        big = ctx.enter_context(tc.tile_pool(name="big", bufs=9))
-        groupp = ctx.enter_context(tc.tile_pool(name="groupp", bufs=4))
+        arena = ctx.enter_context(tc.tile_pool(name="arena", bufs=1))
         qinp = ctx.enter_context(tc.tile_pool(name="qinp", bufs=1))
         qoutp = ctx.enter_context(tc.tile_pool(name="qoutp", bufs=3))
         small = ctx.enter_context(tc.tile_pool(name="small", bufs=2))
@@ -54,6 +56,9 @@ def tile_lowrank_adam_style_step_d7_kernel(
         ps_r = ctx.enter_context(tc.psum_pool(name="ps_r", bufs=2))
         ps_u = ctx.enter_context(tc.psum_pool(name="ps_u", bufs=3))
         ctx.enter_context(tc.manual_schedule())
+
+        def placed(shape, dtype, name, at):
+            return arena.tile(shape, dtype, align_bytes=DMA_ALIGN, name=name, offset=at)
 
         sc_rows = keep.tile([P, 32], F32, align_bytes=64)
         sc_cols = keep.tile([P, 32], F32, align_bytes=64)
@@ -70,39 +75,35 @@ def tile_lowrank_adam_style_step_d7_kernel(
         ident = keep.tile([P, P], F32)
         make_identity(nc, ident[:])
 
-        mom_t, v_t, w_t, o_t, o_pair = {}, {}, {}, {}, {}
-        a_b = [keep.tile([P, N], U8, align_bytes=DMA_ALIGN, name="a_b%d" % t) for t in range(4)]
-        b_b = [keep.tile([P, 2, N], U8, align_bytes=DMA_ALIGN, name="b_b%d" % x) for x in range(2)]
+        mom_t, v_t, w_t, o_t = {}, {}, {}, {}
+        a_b, b_b = {}, {}
 
-        def load_a(t):
-            nc.sync.dma_start(out=a_b[t][:], in_=a_rows[:, t, :])
+        def load_planes(name, rows, at, views, t, end):
+            planes = placed([P, end - t, N], U8, "%s%d" % (name, t), at + N * t)
+            nc.sync.dma_start(out=planes[:], in_=rows[:, t:end, :])
+            for i in range(t, end):
+                views[i] = planes[:, i - t, :]
 
-        def load_b(x):
-            nc.sync.dma_start(out=b_b[x][:], in_=b_rows[:, 2 * x : 2 * x + 2, :])
+        def load_a(t, end):
+            load_planes("a_b", a_rows, B_AT, a_b, t, end)
 
-        def load_mom(k):
-            four = big.tile([P, 4, N], BF16, align_bytes=DMA_ALIGN, name="mom_four", tag="big")
-            nc.sync.dma_start(out=four[:], in_=mom_v[:, k : k + 4, :])
-            for i in range(4):
-                mom_t[k + i] = four[:, i, :]
+        def load_b(t, end):
+            load_planes("b_b", b_rows, B_AT + 6 * KIB, b_b, t, end)
 
-        def load_mom_early(k, n):
-            few = keep.tile([P, n, N], BF16, align_bytes=DMA_ALIGN, name="mom_early%d" % k)
-            nc.sync.dma_start(out=few[:], in_=mom_v[:, k : k + n, :])
-            for i in range(n):
-                mom_t[k + i] = few[:, i, :]
+        def load_rows(name, src, width, at, views, k, end):
+            rows = placed([P, end - k, width], BF16, "%s%d" % (name, k), at + 2 * width * k)
+            nc.sync.dma_start(out=rows[:], in_=src[:, k:end, :])
+            for i in range(k, end):
+                views[i] = rows[:, i - k, :]
 
-        def load_v(k, n):
-            vt = keep.tile([P, n, R], BF16, align_bytes=DMA_ALIGN, name="v_t%d" % k)
-            nc.sync.dma_start(out=vt[:], in_=v_v[:, k : k + n, :])
-            for i in range(n):
-                v_t[k + i] = vt[:, i, :]
+        def load_mom(k, end):
+            load_rows("mom", mom_v, N, MOM_AT, mom_t, k, end)
 
-        def load_w(k):
-            four = big.tile([P, 4, N], BF16, align_bytes=DMA_ALIGN, name="w_four", tag="big")
-            nc.sync.dma_start(out=four[:], in_=w_v[:, k : k + 4, :])
-            for i in range(4):
-                w_t[k + i] = four[:, i, :]
+        def load_v(k, end):
+            load_rows("v", v_v, R, V_AT, v_t, k, end)
+
+        def load_w(k, end):
+            load_rows("w", w_v, N, W_AT, w_t, k, end)
 
         def move(eng, dst, src):
             if eng == "S":
@@ -116,7 +117,7 @@ def tile_lowrank_adam_style_step_d7_kernel(
             else:
                 nc.vector.tensor_scalar(out=dst, in0=src, scalar1=sc, scalar2=None, op0=ALU.mult)
 
-        a_wide = [keep.tile([P, N], BF16, name="a_wide%d" % t, tag="a_wide%d" % t) for t in range(4)]
+        a_wide = [placed([P, N], BF16, "a_wide%d" % t, A_AT + 3 * KIB * t) for t in range(4)]
         a_c = keep.tile([P, GROUPS, R], U32, align_bytes=64)
         a_s = keep.tile([P, GROUPS, R], U8, align_bytes=64)
         a_g, a_bank = {}, {}
@@ -124,26 +125,35 @@ def tile_lowrank_adam_style_step_d7_kernel(
         def widen_a(t):
             for j in range(NBLK):
                 cols = slice(P * j, P * (j + 1))
-                eng = "V" if j < A_ON_VECTOR else "S"
-                scaled(eng, a_wide[t][:, cols], a_b[t][:, cols].bitcast(FP8), a_sc[:, j : j + 1])
+                src = a_b[t][:, cols].bitcast(FP8)
+                if j < A_ON_VECTOR:
+                    g, q = divmod(j, 4)
+                    dst = a_wide[t][:, 512 * g : 512 * (g + 1)].rearrange("p (x n e) -> p n x e", x=2, e=2)
+                    scaled("V", dst[:, 32 * q : 32 * (q + 1)], src.rearrange("p (n x e) -> p n x e", x=2, e=2), a_sc[:, j : j + 1])
+                else:
+                    scaled("S", a_wide[t][:, cols], src, a_sc[:, j : j + 1])
 
         def turn_a(t):
             u, e = divmod(t, 2)
             words = a_wide[t][:].bitcast(F32)
             for g in range(GROUPS):
                 if e == 0:
-                    if u == 1 and g < 2:
+                    if u == 0:
+                        a_bank[g, u] = ps_u.tile([P, 4, P], F32, name="u")
+                    elif g < 2:
                         a_bank[g, u] = ps_r.tile([P, 4, P], F32, name="r")
                     else:
-                        a_bank[g, u] = ps_u.tile([P, 4, P], F32, name="u")
+                        a_bank[g, u] = ps_t.tile([P, 4, P], F32, name="bank")
                 for x in range(2):
-                    nc.tensor.transpose(
-                        a_bank[g, u][:, 2 * e + x, :], words[:, 256 * g + x : 256 * (g + 1) : 2], ident[:]
-                    )
+                    if 4 * g < A_ON_VECTOR:
+                        src = words[:, 256 * g + P * x : 256 * g + P * (x + 1)]
+                    else:
+                        src = words[:, 256 * g + x : 256 * (g + 1) : 2]
+                    nc.tensor.transpose(a_bank[g, u][:, 2 * e + x, :], src, ident[:])
 
         def empty_a(g, u, eng):
             if g not in a_g:
-                a_g[g] = groupp.tile([P, 4 * R], BF16, align_bytes=64, name="a_g", tag="group")
+                a_g[g] = placed([P, 4 * R], BF16, "a_g%d" % g, A_AT + 12 * KIB + 4 * KIB * g)
             words = a_g[g][:].bitcast(F32)
             move(
                 eng,
@@ -154,23 +164,23 @@ def tile_lowrank_adam_style_step_d7_kernel(
         def quant_a(g):
             nc.vector.quantize_mx(out=a_c[:, g, :].bitcast(FP8X4), scales=a_s[:, g, :], in_=a_g[g][:])
 
-        b_wide = keep.tile([P, 4, N], BF16)
+        b_wide = placed([P, 4, N], BF16, "b_wide", B_AT + 12 * KIB)
         b_c = keep.tile([P, N], U32, align_bytes=64)
         b_s = keep.tile([P, N], U8, align_bytes=64)
         b_g = {}
 
         def widen_b(t, eng, cols=slice(0, N)):
-            move(eng, b_wide[:, t, cols], b_b[t // 2][:, t % 2, cols].bitcast(FP8))
+            move(eng, b_wide[:, t, cols], b_b[t][:, cols].bitcast(FP8))
 
         def scale_b(c, js, eng):
             if c not in b_g:
-                b_g[c] = groupp.tile([P, 512, 4], BF16, align_bytes=64, name="b_g", tag="group")
+                b_g[c] = placed([P, 512, 4], BF16, "b_g%d" % c, BG_AT + 4 * KIB * c)
             for j in js:
                 jj = 4 * c + j
                 scaled(
                     eng,
-                    b_g[c][:, P * j : P * (j + 1), :],
-                    b_wide[:, :, P * jj : P * (jj + 1)].rearrange("p t n -> p n t"),
+                    b_g[c][:, P * j : P * (j + 1), :].rearrange("p (m i) t -> p m t i", i=4),
+                    b_wide[:, :, P * jj : P * (jj + 1)].rearrange("p t (m i) -> p m t i", i=4),
                     b_sc[:, jj : jj + 1],
                 )
 
@@ -183,15 +193,17 @@ def tile_lowrank_adam_style_step_d7_kernel(
             )
 
         srt, rs, h, r_bank, r_sb, u_bank = {}, {}, {}, {}, {}, {}
-        bank_x, bank_y, q_in, q_c, q_s = {}, {}, {}, {}, {}
+        bank_x, bank_y, q_in, q_c, q_s, u_sb, done = {}, {}, {}, {}, {}, {}, {}
 
         def parts(s):
             return (0 if s + AHEAD < TILES else 3), (4 if s >= 0 else 3)
 
-        def sort_mom(k):
-            srt[k] = small.tile([P, SORTED, 2, P], F32, name="srt")
-            words = mom_t[k].bitcast(F32)[:, 0 : 256 * SORTED]
-            nc.scalar.copy(out=srt[k][:], in_=words.rearrange("p (g n x) -> p g x n", g=SORTED, x=2))
+        def sort_mom(k, g, n, eng):
+            words = small.tile([P, n, 2, P], F32, name="srt%d" % g, bufs=3)
+            src = mom_t[k].bitcast(F32)[:, 256 * g : 256 * (g + n)]
+            move(eng, words[:], src.rearrange("p (g n x) -> p g x n", g=n, x=2))
+            for i in range(n):
+                srt[k, g + i] = words[:, i]
 
         def inv_root(k):
             rs[k] = rsp.tile([P, 2, P, 2], F32, name="rs")
@@ -201,16 +213,16 @@ def tile_lowrank_adam_style_step_d7_kernel(
                 func=ACT.Abs_reciprocal_sqrt,
             )
 
-        def turn_mom(s):
+        def turn_mom(s, pool=ps_t, tag="bank"):
             k = s + AHEAD
             words = mom_t[k].bitcast(F32)
-            bank_x[s] = ps_t.tile([P, 4, P], F32, name="bank")
-            bank_y[s] = ps_t.tile([P, 4, P], F32, name="bank")
+            bank_x[s] = pool.tile([P, 4, P], F32, name=tag)
+            bank_y[s] = pool.tile([P, 4, P], F32, name=tag)
             for g in range(GROUPS):
                 for x in range(2):
                     dst = bank_x[s][:, 2 * g + x, :] if g < 2 else bank_y[s][:, x, :]
-                    if k in srt and g < SORTED:
-                        src = srt[k][:, g, x, :]
+                    if (k, g) in srt:
+                        src = srt[k, g][:, x, :]
                     else:
                         src = words[:, 256 * g + x : 256 * (g + 1) : 2]
                     nc.tensor.transpose(dst, src, ident[:])
@@ -222,20 +234,27 @@ def tile_lowrank_adam_style_step_d7_kernel(
             for x in range(2):
                 nc.tensor.transpose(bank_y[s][:, 2 + x, :], words[:, P * x : P * (x + 1)], ident[:])
 
-        def empty(s):
-            lo, hi = parts(s)
+        def empty_x(s):
             slot = s % Q_SLOTS
             q_in[s] = qinp.tile(
                 [P, 4, 512], BF16, align_bytes=64, name="q_in%d" % slot, offset=4096 * slot
             )
-            words = q_in[s][:].bitcast(F32).rearrange("p a (n x) -> p a n x", x=2)
-            if lo == 0:
+            if parts(s)[0] == 0:
+                words = q_in[s][:].bitcast(F32).rearrange("p a (n x) -> p a n x", x=2)
                 nc.scalar.copy(out=words[:, 0:2], in_=bank_x[s][:].rearrange("p (a x) n -> p a n x", x=2))
+
+        def empty_y(s):
+            lo, hi = parts(s)
             lo = max(lo, 2)
+            words = q_in[s][:].bitcast(F32).rearrange("p a (n x) -> p a n x", x=2)
             nc.scalar.copy(
                 out=words[:, lo:hi],
                 in_=bank_y[s][:].rearrange("p (a x) n -> p a n x", x=2)[:, lo - 2 : hi - 2],
             )
+
+        def empty(s):
+            empty_x(s)
+            empty_y(s)
 
         def quant(s):
             lo, hi = parts(s)
@@ -270,11 +289,11 @@ def tile_lowrank_adam_style_step_d7_kernel(
             )
 
         def fetch_r(k):
-            r_sb[k] = keep.tile([P, R], F32, name="r_sb", tag="a_wide0")
+            r_sb[k] = small.tile([P, R], F32, name="r_sb")
             nc.scalar.copy(out=r_sb[k][:], in_=r_bank[k][:])
 
-        def direction_gpsimd(k):
-            slot = (k - 2) % Q_SLOTS
+        def direction_gpsimd(k, s):
+            slot = s % Q_SLOTS
             h[k] = qinp.tile([P, R], BF16, align_bytes=64, name="h%d" % slot, offset=4096 * slot + 3072)
             nc.gpsimd.tensor_tensor(
                 out=h[k][:],
@@ -296,45 +315,69 @@ def tile_lowrank_adam_style_step_d7_kernel(
                 stop=True,
             )
 
+        def out_rows(k, c):
+            if k not in o_t:
+                end = min([e for e in OUT_AT if e > k] + [TILES])
+                rows = placed([P, end - k, N], F32, "out%d" % k, OUT_AT[k])
+                for i in range(k, end):
+                    o_t[i] = (rows, k)
+            rows, base = o_t[k]
+            return rows[:, k - base, 512 * c : 512 * (c + 1)]
+
         def finish(k, c):
             cols = slice(512 * c, 512 * (c + 1))
-            if k % 2 == 0 and c == 0:
-                o_pair[k] = big.tile([P, 2, N], F32, align_bytes=DMA_ALIGN, name="o_pair", tag="big")
-                o_t[k], o_t[k + 1] = o_pair[k][:, 0, :], o_pair[k][:, 1, :]
             nc.vector.scalar_tensor_tensor(
-                out=o_t[k][:, cols],
+                out=out_rows(k, c),
                 in0=w_t[k][:, cols],
                 scalar=KEEP,
                 in1=u_bank[k, c][:],
                 op0=ALU.mult,
                 op1=ALU.subtract,
             )
-            if k >= CHUNKED:
-                nc.sync.dma_start(out=out_v[:, k, cols], in_=o_t[k][:, cols])
-            elif c == CHUNKS - 1 and k >= PAIRED:
-                nc.sync.dma_start(out=out_v[:, k, :], in_=o_t[k])
-            elif c == CHUNKS - 1 and k % 2 == 1:
-                nc.sync.dma_start(out=out_v[:, k - 1 : k + 1, :], in_=o_pair[k - 1][:])
+            store(k, c)
+
+        def decay(k, c):
+            nc.scalar.activation(
+                out=out_rows(k, c), in_=w_t[k][:, 512 * c : 512 * (c + 1)], func=ACT.Copy, scale=KEEP
+            )
+
+        def fetch_u(k, c, s):
+            slot = s % Q_SLOTS
+            u_sb[k] = qinp.tile([P, 512], F32, align_bytes=64, name="u%d" % slot, offset=4096 * slot + 2048)
+            nc.scalar.copy(out=u_sb[k][:], in_=u_bank[k, c][:])
+
+        def finish_gpsimd(k, c):
+            nc.gpsimd.tensor_tensor(out=out_rows(k, c), in0=out_rows(k, c), in1=u_sb[k][:], op=ALU.subtract)
+            store(k, c)
+
+        def store(k, c):
+            rows, base = o_t[k]
+            done.setdefault(k, set()).add(c)
+            if k in PIECES:
+                for lo, hi in PIECES[k]:
+                    if lo <= c < hi and all(i in done[k] for i in range(lo, hi)):
+                        cols = slice(512 * lo, 512 * hi)
+                        nc.sync.dma_start(out=out_v[:, k, cols], in_=rows[:, k - base, cols])
+            elif len(done[k]) == CHUNKS and k + 1 in STORES:
+                first = STORES[STORES.index(k + 1) - 1]
+                nc.sync.dma_start(out=out_v[:, first : k + 1, :], in_=rows[:, first - base : k - base + 1, :])
 
         load_v(0, 1)
         for t in range(4):
-            load_a(t)
-        load_b(0)
-        load_mom_early(0, 1)
-        load_b(1)
-        load_mom_early(1, 1)
-        load_v(1, 3)
-        load_mom_early(2, 2)
-        load_mom(4)
-        load_v(4, 4)
-        load_w(0)
-        load_mom(8)
-        load_v(8, 8)
-        load_w(4)
-        load_mom(12)
-        load_w(8)
-        load_w(12)
-
+            load_a(t, t + 1)
+        load_b(0, 2)
+        load_mom(0, 1)
+        load_b(2, 4)
+        load_mom(1, 2)
+        load_v(1, 6)
+        load_mom(2, 4)
+        load_mom(4, 8)
+        load_w(0, 4)
+        load_v(6, 16)
+        load_mom(8, 12)
+        load_w(4, 8)
+        load_mom(12, 16)
+        load_w(8, 16)
         inv_root(0)
         for t in range(4):
             widen_a(t)
@@ -385,8 +428,6 @@ def tile_lowrank_adam_style_step_d7_kernel(
         scale_b(2, range(3, 4), "S")
         inv_root(3)
 
-        def on_gpsimd(k):
-            return 4 <= k < TILES and (k % 2 == 0 or k + AHEAD >= TILES)
 
         quant(0)
         project(3)
@@ -395,7 +436,7 @@ def tile_lowrank_adam_style_step_d7_kernel(
         turn_mom(2)
         turn_h(2)
         empty(2)
-        sort_mom(6)
+        sort_mom(6, 0, 2, "S")
         inv_root(4)
         scale_b(1, range(2, 4), "V")
         quant(1)
@@ -411,10 +452,11 @@ def tile_lowrank_adam_style_step_d7_kernel(
                 direction(3)
         turn_mom(3)
         turn_h(3)
-        sort_mom(7)
+        sort_mom(7, 0, 2, "S")
         fetch_r(4)
         inv_root(5)
         empty(3)
+
 
         for s in range(2, TILES + 1):
             late = s + AHEAD > TILES
@@ -422,20 +464,20 @@ def tile_lowrank_adam_style_step_d7_kernel(
                 finish(s - 1, 0)
             if s < TILES:
                 quant(s)
+            if s + 2 + AHEAD < TILES:
+                sort_mom(s + 2 + AHEAD, 3 - 1, 1, "V")
             if s + AHEAD < TILES:
                 project(s + AHEAD)
-            if on_gpsimd(s + 2):
-                direction_gpsimd(s + 2)
+            if s + 2 < TILES:
+                direction_gpsimd(s + 2, s)
             for c in range(CHUNKS):
                 if c > 0 or not late:
                     finish(s - 1, c)
                 if s < TILES:
                     lift(s, c)
-            if s + 2 < TILES and not on_gpsimd(s + 2):
-                direction(s + 2)
             if s + 3 + AHEAD < TILES:
-                sort_mom(s + 3 + AHEAD)
-            if on_gpsimd(s + 3):
+                sort_mom(s + 3 + AHEAD, 0, 1, "S")
+            if s + 3 < TILES:
                 fetch_r(s + 3)
             if s + 4 < TILES:
                 inv_root(s + 4)

@@ -465,7 +465,7 @@ def tile_lowrank_adam_style_step_d7_kernel(
             if s < TILES:
                 quant(s)
             if s + 2 + AHEAD < TILES:
-                sort_mom(s + 2 + AHEAD, 3 - 1, 1, "V")
+                sort_mom(s + 2 + AHEAD, 3 - 2, 2, "V")
             if s + AHEAD < TILES:
                 project(s + AHEAD)
             if s + 2 < TILES:

@@ -30,8 +30,8 @@ KIB = 1024
 MOM_AT, W_AT, V_AT = 0, 48 * KIB, 96 * KIB
 A_AT, B_AT, BG_AT = 112 * KIB, 136 * KIB, 160 * KIB
 OUT_AT = {0: A_AT, 4: B_AT, 7: MOM_AT, 11: MOM_AT + 24 * KIB}
-STORES = (0, 4, 7, 9, 10, 11, 12, 13)
-PIECES = {13: ((0, 2), (2, 3)), 14: ((0, 2), (2, 3)), 15: ((0, 1), (1, 2), (2, 3))}
+STORES = (0, 4, 7, 9, 10, 11)
+PIECES = {11: ((0, 2), (2, 3)), 12: ((0, 1), (1, 2), (2, 3)), 13: ((0, 1), (1, 2), (2, 3)), 14: ((0, 1), (1, 2), (2, 3)), 15: ((0, 1), (1, 2), (2, 3))}
 
 
 def tile_lowrank_adam_style_step_d7_kernel(
@@ -54,7 +54,7 @@ def tile_lowrank_adam_style_step_d7_kernel(
         rsp = ctx.enter_context(tc.tile_pool(name="rsp", bufs=3))
         ps_t = ctx.enter_context(tc.psum_pool(name="ps_t", bufs=3))
         ps_r = ctx.enter_context(tc.psum_pool(name="ps_r", bufs=2))
-        ps_u = ctx.enter_context(tc.psum_pool(name="ps_u", bufs=3))
+        ps_u = ctx.enter_context(tc.psum_pool(name="ps_u", bufs=1))
         ctx.enter_context(tc.manual_schedule())
 
         def placed(shape, dtype, name, at):
@@ -64,7 +64,7 @@ def tile_lowrank_adam_style_step_d7_kernel(
         sc_cols = keep.tile([P, 32], F32, align_bytes=64)
         sc_wide = keep.tile([P, 32], F32, align_bytes=64)
         sc_all = keep.tile([P, 32], F32, align_bytes=64)
-        nc.gpsimd.memset(sc_rows[:], 0.0)
+        nc.vector.memset(sc_rows[:], 0.0)
         nc.scalar.dma_start(out=sc_rows[0:P:32, 0:NBLK], in_=a_scale)
         nc.scalar.dma_start(out=sc_rows[0:P:32, 16 : 16 + NBLK], in_=b_scale)
         nc.vector.transpose(out=sc_cols[:], in_=sc_rows[:])
@@ -126,12 +126,8 @@ def tile_lowrank_adam_style_step_d7_kernel(
             for j in range(NBLK):
                 cols = slice(P * j, P * (j + 1))
                 src = a_b[t][:, cols].bitcast(FP8)
-                if j < A_ON_VECTOR:
-                    g, q = divmod(j, 4)
-                    dst = a_wide[t][:, 512 * g : 512 * (g + 1)].rearrange("p (x n e) -> p n x e", x=2, e=2)
-                    scaled("V", dst[:, 32 * q : 32 * (q + 1)], src.rearrange("p (n x e) -> p n x e", x=2, e=2), a_sc[:, j : j + 1])
-                else:
-                    scaled("S", a_wide[t][:, cols], src, a_sc[:, j : j + 1])
+                eng = "V" if j < A_ON_VECTOR else "S"
+                scaled(eng, a_wide[t][:, cols], src, a_sc[:, j : j + 1])
 
         def turn_a(t):
             u, e = divmod(t, 2)
@@ -139,16 +135,13 @@ def tile_lowrank_adam_style_step_d7_kernel(
             for g in range(GROUPS):
                 if e == 0:
                     if u == 0:
-                        a_bank[g, u] = ps_u.tile([P, 4, P], F32, name="u")
+                        a_bank[g, u] = ps_u.tile([P, 4, P], F32, name="u%d" % g)
                     elif g < 2:
                         a_bank[g, u] = ps_r.tile([P, 4, P], F32, name="r")
                     else:
                         a_bank[g, u] = ps_t.tile([P, 4, P], F32, name="bank")
                 for x in range(2):
-                    if 4 * g < A_ON_VECTOR:
-                        src = words[:, 256 * g + P * x : 256 * g + P * (x + 1)]
-                    else:
-                        src = words[:, 256 * g + x : 256 * (g + 1) : 2]
+                    src = words[:, 256 * g + x : 256 * (g + 1) : 2]
                     nc.tensor.transpose(a_bank[g, u][:, 2 * e + x, :], src, ident[:])
 
         def empty_a(g, u, eng):
@@ -304,7 +297,7 @@ def tile_lowrank_adam_style_step_d7_kernel(
 
         def lift(k, c):
             cols = slice(512 * c, 512 * (c + 1))
-            u_bank[k, c] = ps_u.tile([P, 512], F32, name="u")
+            u_bank[k, c] = ps_u.tile([P, 512], F32, name="u%d" % c)
             nc.tensor.matmul_mx(
                 out=u_bank[k, c][:],
                 lhsT=q_c[k][:, 3, :].bitcast(FP8X4),
@@ -363,8 +356,8 @@ def tile_lowrank_adam_style_step_d7_kernel(
                 nc.sync.dma_start(out=out_v[:, first : k + 1, :], in_=rows[:, first - base : k - base + 1, :])
 
         load_v(0, 1)
-        for t in range(4):
-            load_a(t, t + 1)
+        load_a(0, 2)
+        load_a(2, 4)
         load_b(0, 2)
         load_mom(0, 1)
         load_b(2, 4)
@@ -400,10 +393,11 @@ def tile_lowrank_adam_style_step_d7_kernel(
         quant_a(1)
         quant_a(2)
         empty(-2)
-        widen_b(3, "S")
+        widen_b(3, "S", slice(0, 512))
         project(0)
         turn_mom(-1)
         quant(-2)
+        widen_b(3, "V", slice(512, N))
         scale_b(0, range(0, 2), "V")
         direction(0)
         inv_root(1)
@@ -445,18 +439,23 @@ def tile_lowrank_adam_style_step_d7_kernel(
         lift(0, 1)
         quant_b(2)
         lift(0, 2)
-        for c in range(CHUNKS):
-            finish(0, c)
-            lift(1, c)
-            if c == 0:
-                direction(3)
+        finish(0, 0)
+        lift(1, 0)
+        direction(3)
+        finish(0, 1)
+        lift(1, 1)
         turn_mom(3)
         turn_h(3)
-        sort_mom(7, 0, 2, "S")
+        finish(0, 2)
+        lift(1, 2)
+        sort_mom(7, 0, 1, "S")
         fetch_r(4)
         inv_root(5)
         empty(3)
 
+
+        def on_gpsimd(k):
+            return 4 <= k < TILES and (True)
 
         for s in range(2, TILES + 1):
             late = s + AHEAD > TILES
@@ -468,21 +467,24 @@ def tile_lowrank_adam_style_step_d7_kernel(
                 sort_mom(s + 2 + AHEAD, 3 - 2, 2, "V")
             if s + AHEAD < TILES:
                 project(s + AHEAD)
-            if s + 2 < TILES:
+            if on_gpsimd(s + 2):
                 direction_gpsimd(s + 2, s)
+            elif s + 2 < TILES:
+                direction(s + 2)
             for c in range(CHUNKS):
+                if c == 2:
+                    if s + 3 + AHEAD < TILES:
+                        sort_mom(s + 3 + AHEAD, 0, 1, "S")
+                    if on_gpsimd(s + 3):
+                        fetch_r(s + 3)
+                    if s + 4 < TILES:
+                        inv_root(s + 4)
+                    if s + 2 + AHEAD < TILES:
+                        turn_mom(s + 2)
+                    if s + 2 < TILES:
+                        turn_h(s + 2)
+                        empty(s + 2)
                 if c > 0 or not late:
                     finish(s - 1, c)
                 if s < TILES:
                     lift(s, c)
-            if s + 3 + AHEAD < TILES:
-                sort_mom(s + 3 + AHEAD, 0, 1, "S")
-            if s + 3 < TILES:
-                fetch_r(s + 3)
-            if s + 4 < TILES:
-                inv_root(s + 4)
-            if s + 2 + AHEAD < TILES:
-                turn_mom(s + 2)
-            if s + 2 < TILES:
-                turn_h(s + 2)
-                empty(s + 2)

@@ -64,7 +64,7 @@ def tile_lowrank_adam_style_step_d7_kernel(
         sc_cols = keep.tile([P, 32], F32, align_bytes=64)
         sc_wide = keep.tile([P, 32], F32, align_bytes=64)
         sc_all = keep.tile([P, 32], F32, align_bytes=64)
-        nc.vector.memset(sc_rows[:], 0.0)
+        nc.gpsimd.memset(sc_rows[:], 0.0)
         nc.scalar.dma_start(out=sc_rows[0:P:32, 0:NBLK], in_=a_scale)
         nc.scalar.dma_start(out=sc_rows[0:P:32, 16 : 16 + NBLK], in_=b_scale)
         nc.vector.transpose(out=sc_cols[:], in_=sc_rows[:])
@@ -126,8 +126,12 @@ def tile_lowrank_adam_style_step_d7_kernel(
             for j in range(NBLK):
                 cols = slice(P * j, P * (j + 1))
                 src = a_b[t][:, cols].bitcast(FP8)
-                eng = "V" if j < A_ON_VECTOR else "S"
-                scaled(eng, a_wide[t][:, cols], src, a_sc[:, j : j + 1])
+                if j < A_ON_VECTOR:
+                    g, q = divmod(j, 4)
+                    dst = a_wide[t][:, 512 * g : 512 * (g + 1)].rearrange("p (x n e) -> p n x e", x=2, e=2)
+                    scaled("V", dst[:, 32 * q : 32 * (q + 1)], src.rearrange("p (n x e) -> p n x e", x=2, e=2), a_sc[:, j : j + 1])
+                else:
+                    scaled("S", a_wide[t][:, cols], src, a_sc[:, j : j + 1])
 
         def turn_a(t):
             u, e = divmod(t, 2)
@@ -141,7 +145,10 @@ def tile_lowrank_adam_style_step_d7_kernel(
                     else:
                         a_bank[g, u] = ps_t.tile([P, 4, P], F32, name="bank")
                 for x in range(2):
-                    src = words[:, 256 * g + x : 256 * (g + 1) : 2]
+                    if 4 * g < A_ON_VECTOR:
+                        src = words[:, 256 * g + P * x : 256 * g + P * (x + 1)]
+                    else:
+                        src = words[:, 256 * g + x : 256 * (g + 1) : 2]
                     nc.tensor.transpose(a_bank[g, u][:, 2 * e + x, :], src, ident[:])
 
         def empty_a(g, u, eng):
@@ -356,8 +363,8 @@ def tile_lowrank_adam_style_step_d7_kernel(
                 nc.sync.dma_start(out=out_v[:, first : k + 1, :], in_=rows[:, first - base : k - base + 1, :])
 
         load_v(0, 1)
-        load_a(0, 2)
-        load_a(2, 4)
+        for t in range(4):
+            load_a(t, t + 1)
         load_b(0, 2)
         load_mom(0, 1)
         load_b(2, 4)

@@ -30,8 +30,8 @@ KIB = 1024
 MOM_AT, W_AT, V_AT = 0, 48 * KIB, 96 * KIB
 A_AT, B_AT, BG_AT = 112 * KIB, 136 * KIB, 160 * KIB
 OUT_AT = {0: A_AT, 4: B_AT, 7: MOM_AT, 11: MOM_AT + 24 * KIB}
-STORES = (0, 4, 7, 9, 10, 11)
-PIECES = {11: ((0, 2), (2, 3)), 12: ((0, 1), (1, 2), (2, 3)), 13: ((0, 1), (1, 2), (2, 3)), 14: ((0, 1), (1, 2), (2, 3)), 15: ((0, 1), (1, 2), (2, 3))}
+STORES = (0, 4, 7, 9, 10, 11, 12, 13)
+PIECES = {13: ((0, 2), (2, 3)), 14: ((0, 2), (2, 3)), 15: ((0, 2), (2, 3))}
 
 
 def tile_lowrank_adam_style_step_d7_kernel(
@@ -293,8 +293,11 @@ def tile_lowrank_adam_style_step_d7_kernel(
             nc.scalar.copy(out=r_sb[k][:], in_=r_bank[k][:])
 
         def direction_gpsimd(k, s):
-            slot = s % Q_SLOTS
-            h[k] = qinp.tile([P, R], BF16, align_bytes=64, name="h%d" % slot, offset=4096 * slot + 3072)
+            if s is None:
+                h[k] = placed([P, R], BF16, "h_first", BG_AT + 4 * KIB)
+            else:
+                slot = s % Q_SLOTS
+                h[k] = qinp.tile([P, R], BF16, align_bytes=64, name="h%d" % slot, offset=4096 * slot + 3072)
             nc.gpsimd.tensor_tensor(
                 out=h[k][:],
                 in0=r_sb[k][:],
@@ -369,8 +372,8 @@ def tile_lowrank_adam_style_step_d7_kernel(
         load_mom(0, 1)
         load_b(2, 4)
         load_mom(1, 2)
-        load_v(1, 6)
         load_mom(2, 4)
+        load_v(1, 6)
         load_mom(4, 8)
         load_w(0, 4)
         load_v(6, 16)
@@ -400,66 +403,63 @@ def tile_lowrank_adam_style_step_d7_kernel(
         quant_a(1)
         quant_a(2)
         empty(-2)
-        widen_b(3, "S", slice(0, 512))
-        project(0)
         turn_mom(-1)
+        widen_b(3, "S", slice(0, 512))
+        widen_b(3, "S", slice(1024, N))
+        project(0)
         quant(-2)
-        widen_b(3, "V", slice(512, N))
-        scale_b(0, range(0, 2), "V")
-        direction(0)
-        inv_root(1)
-        scale_b(2, range(0, 1), "S")
-        empty(-1)
         project(1)
+        empty(-1)
+        inv_root(1)
+        inv_root(2)
+        widen_b(3, "V", slice(512, 1024))
+        scale_b(0, range(0, 2), "V")
+        quant(-1)
+        direction(0)
         turn_mom(0)
         turn_h(0)
-        scale_b(0, range(2, 4), "V")
-        quant(-1)
         project(2)
-        scale_b(2, range(1, 2), "S")
+        scale_b(2, range(0, 2), "S")
         empty(0)
+        scale_b(0, range(2, 4), "V")
         direction(1)
-        quant_b(0)
-        scale_b(1, range(0, 2), "V")
-        inv_root(2)
         turn_mom(1)
         turn_h(1)
-        scale_b(2, range(2, 3), "S")
+        scale_b(2, range(2, 4), "S")
         empty(1)
-        scale_b(2, range(3, 4), "S")
-        inv_root(3)
-
-
+        quant_b(0)
+        scale_b(1, range(0, 2), "V")
         quant(0)
         project(3)
         lift(0, 0)
         direction(2)
         turn_mom(2)
         turn_h(2)
+        inv_root(3)
+        fetch_r(3)
         empty(2)
-        sort_mom(6, 0, 2, "S")
-        inv_root(4)
         scale_b(1, range(2, 4), "V")
+        quant_b(2)
+        lift(0, 2)
         quant(1)
         project(4)
         quant_b(1)
         lift(0, 1)
-        quant_b(2)
-        lift(0, 2)
+        sort_mom(6, 1, 2, "V")
+        direction_gpsimd(3, None)
+        inv_root(4)
         finish(0, 0)
         lift(1, 0)
-        direction(3)
-        finish(0, 1)
-        lift(1, 1)
-        turn_mom(3)
-        turn_h(3)
         finish(0, 2)
         lift(1, 2)
-        sort_mom(7, 0, 1, "S")
+        turn_mom(3)
+        turn_h(3)
+        finish(0, 1)
+        lift(1, 1)
         fetch_r(4)
+        sort_mom(7, 0, 1, "S")
         inv_root(5)
         empty(3)
-
 
         def on_gpsimd(k):
             return 4 <= k < TILES and (True)

@@ -29,9 +29,9 @@ A_ON_VECTOR = 8
 KIB = 1024
 MOM_AT, W_AT, V_AT = 0, 48 * KIB, 96 * KIB
 A_AT, B_AT, BG_AT = 112 * KIB, 136 * KIB, 160 * KIB
-OUT_AT = {0: A_AT, 4: B_AT, 7: MOM_AT, 11: MOM_AT + 24 * KIB}
-STORES = (0, 4, 7, 9, 10, 11, 12, 13)
-PIECES = {13: ((0, 2), (2, 3)), 14: ((0, 2), (2, 3)), 15: ((0, 2), (2, 3))}
+OUT_AT = {0: A_AT, 3: B_AT, 6: MOM_AT, 11: MOM_AT + 30 * KIB}
+STORES = (0, 3, 6, 9, 11, 12, 13, 14, 15, 16)
+PIECES = {}
 
 
 def tile_lowrank_adam_style_step_d7_kernel(

@@ -28,7 +28,7 @@ DMA_ALIGN = 256
 A_ON_VECTOR = 8
 KIB = 1024
 MOM_AT, W_AT, V_AT = 0, 48 * KIB, 96 * KIB
-A_AT, B_AT, BG_AT = 112 * KIB, 136 * KIB, 160 * KIB
+A_AT, B_AT, BG_AT = 112 * KIB, 136 * KIB, 161 * KIB
 OUT_AT = {0: A_AT, 3: B_AT, 6: MOM_AT, 11: MOM_AT + 30 * KIB}
 STORES = (0, 3, 6, 9, 11, 12, 13, 14, 15, 16)
 PIECES = {}
@@ -67,9 +67,15 @@ def tile_lowrank_adam_style_step_d7_kernel(
         nc.gpsimd.memset(sc_rows[:], 0.0)
         nc.scalar.dma_start(out=sc_rows[0:P:32, 0:NBLK], in_=a_scale)
         nc.scalar.dma_start(out=sc_rows[0:P:32, 16 : 16 + NBLK], in_=b_scale)
-        nc.vector.transpose(out=sc_cols[:], in_=sc_rows[:])
-        nc.vector.tensor_copy(out=sc_wide[:], in_=sc_cols[:, 0:1].to_broadcast([P, 32]))
-        nc.vector.transpose(out=sc_all[:], in_=sc_wide[:])
+
+        def spread_scales(step):
+            if step == 0:
+                nc.vector.transpose(out=sc_cols[:], in_=sc_rows[:])
+            elif step == 1:
+                nc.vector.tensor_copy(out=sc_wide[:], in_=sc_cols[:, 0:1].to_broadcast([P, 32]))
+            else:
+                nc.vector.transpose(out=sc_all[:], in_=sc_wide[:])
+
         a_sc = sc_all[:, 0:NBLK]
         b_sc = sc_all[:, 16 : 16 + NBLK]
         ident = keep.tile([P, P], F32)
@@ -78,17 +84,17 @@ def tile_lowrank_adam_style_step_d7_kernel(
         mom_t, v_t, w_t, o_t = {}, {}, {}, {}
         a_b, b_b = {}, {}
 
-        def load_planes(name, rows, at, views, t, end):
-            planes = placed([P, end - t, N], U8, "%s%d" % (name, t), at + N * t)
-            nc.sync.dma_start(out=planes[:], in_=rows[:, t:end, :])
+        def load_planes(name, rows, at, views, t, end, pad=0):
+            planes = placed([P, end - t, N + pad], U8, "%s%d" % (name, t), at + N * t)
+            nc.sync.dma_start(out=planes[:, :, 0:N], in_=rows[:, t:end, :])
             for i in range(t, end):
-                views[i] = planes[:, i - t, :]
+                views[i] = planes[:, i - t, 0:N]
 
         def load_a(t, end):
             load_planes("a_b", a_rows, B_AT, a_b, t, end)
 
-        def load_b(t, end):
-            load_planes("b_b", b_rows, B_AT + 6 * KIB, b_b, t, end)
+        def load_b(t, end, pad=0):
+            load_planes("b_b", b_rows, B_AT + 6 * KIB, b_b, t, end, pad)
 
         def load_rows(name, src, width, at, views, k, end):
             rows = placed([P, end - k, width], BF16, "%s%d" % (name, k), at + 2 * width * k)
@@ -164,7 +170,7 @@ def tile_lowrank_adam_style_step_d7_kernel(
         def quant_a(g):
             nc.vector.quantize_mx(out=a_c[:, g, :].bitcast(FP8X4), scales=a_s[:, g, :], in_=a_g[g][:])
 
-        b_wide = placed([P, 4, N], BF16, "b_wide", B_AT + 12 * KIB)
+        b_wide = placed([P, 4, N], BF16, "b_wide", B_AT + 13 * KIB)
         b_c = keep.tile([P, N], U32, align_bytes=64)
         b_s = keep.tile([P, N], U8, align_bytes=64)
         b_g = {}
@@ -213,11 +219,11 @@ def tile_lowrank_adam_style_step_d7_kernel(
                 func=ACT.Abs_reciprocal_sqrt,
             )
 
-        def turn_mom(s, pool=ps_t, tag="bank"):
+        def turn_mom(s, pool=ps_t, tags=("bank", "bank")):
             k = s + AHEAD
             words = mom_t[k].bitcast(F32)
-            bank_x[s] = pool.tile([P, 4, P], F32, name=tag)
-            bank_y[s] = pool.tile([P, 4, P], F32, name=tag)
+            bank_x[s] = pool.tile([P, 4, P], F32, name=tags[0])
+            bank_y[s] = pool.tile([P, 4, P], F32, name=tags[1])
             for g in range(GROUPS):
                 for x in range(2):
                     dst = bank_x[s][:, 2 * g + x, :] if g < 2 else bank_y[s][:, x, :]
@@ -366,8 +372,10 @@ def tile_lowrank_adam_style_step_d7_kernel(
                 nc.sync.dma_start(out=out_v[:, first : k + 1, :], in_=rows[:, first - base : k - base + 1, :])
 
         load_v(0, 1)
-        for t in range(4):
-            load_a(t, t + 1)
+        load_a(0, 1)
+        load_a(1, 2)
+        load_a(2, 3)
+        load_a(3, 4)
         load_b(0, 2)
         load_mom(0, 1)
         load_b(2, 4)
@@ -382,6 +390,8 @@ def tile_lowrank_adam_style_step_d7_kernel(
         load_mom(12, 16)
         load_w(8, 16)
         inv_root(0)
+        for step in range(3):
+            spread_scales(step)
         for t in range(4):
             widen_a(t)
         turn_a(0)
@@ -389,32 +399,32 @@ def tile_lowrank_adam_style_step_d7_kernel(
         for g in range(GROUPS):
             empty_a(g, 0, "S")
         turn_a(2)
-        turn_mom(-3)
         turn_a(3)
-        empty(-3)
-        for t in range(3):
-            widen_b(t, "V")
-        empty_a(0, 1, "V")
+        turn_mom(-3)
+        widen_b(0, "V")
+        widen_b(1, "V")
         empty_a(1, 1, "S")
+        empty_a(0, 1, "V")
         empty_a(2, 1, "S")
-        quant(-3)
-        turn_mom(-2)
-        quant_a(0)
+        turn_mom(-2, ps_u, ("u0", "u1"))
+        empty(-3)
         quant_a(1)
+        quant_a(0)
         quant_a(2)
-        empty(-2)
+        quant(-3)
         turn_mom(-1)
-        widen_b(3, "S", slice(0, 512))
-        widen_b(3, "S", slice(1024, N))
+        empty(-2)
         project(0)
+        widen_b(2, "V")
         quant(-2)
         project(1)
+        widen_b(3, "S", slice(1024, N))
         empty(-1)
         inv_root(1)
         inv_root(2)
-        widen_b(3, "V", slice(512, 1024))
-        scale_b(0, range(0, 2), "V")
+        widen_b(3, "V", slice(0, 1024))
         quant(-1)
+        scale_b(0, range(0, 2), "V")
         direction(0)
         turn_mom(0)
         turn_h(0)

@@ -64,12 +64,16 @@ def tile_lowrank_adam_style_step_d7_kernel(
         sc_cols = keep.tile([P, 32], F32, align_bytes=64)
         sc_wide = keep.tile([P, 32], F32, align_bytes=64)
         sc_all = keep.tile([P, 32], F32, align_bytes=64)
+        sc_in = keep.tile([P, 2, 16], F32, align_bytes=64)
+        nc.scalar.dma_start(out=sc_in[0:P:32, 0, 0:NBLK], in_=a_scale)
+        nc.scalar.dma_start(out=sc_in[0:P:32, 1, 0:NBLK], in_=b_scale)
         nc.gpsimd.memset(sc_rows[:], 0.0)
-        nc.scalar.dma_start(out=sc_rows[0:P:32, 0:NBLK], in_=a_scale)
-        nc.scalar.dma_start(out=sc_rows[0:P:32, 16 : 16 + NBLK], in_=b_scale)
 
         def spread_scales(step):
             if step == 0:
+                for q in range(0, P, 32):
+                    rows = sc_rows[q : q + 1].rearrange("p (a j) -> p a j", a=2)
+                    nc.vector.tensor_copy(out=rows[:, :, 0:NBLK], in_=sc_in[q : q + 1, :, 0:NBLK])
                 nc.vector.transpose(out=sc_cols[:], in_=sc_rows[:])
             elif step == 1:
                 nc.vector.tensor_copy(out=sc_wide[:], in_=sc_cols[:, 0:1].to_broadcast([P, 32]))

@@ -69,11 +69,12 @@ def tile_lowrank_adam_style_step_d7_kernel(
         nc.scalar.dma_start(out=sc_in[0:P:32, 1, 0:NBLK], in_=b_scale)
         nc.gpsimd.memset(sc_rows[:], 0.0)
 
+        for q in range(0, P, 32):
+            rows = sc_rows[q : q + 1].rearrange("p (a j) -> p a j", a=2)
+            nc.vector.tensor_copy(out=rows[:, :, 0:NBLK], in_=sc_in[q : q + 1, :, 0:NBLK])
+
         def spread_scales(step):
             if step == 0:
-                for q in range(0, P, 32):
-                    rows = sc_rows[q : q + 1].rearrange("p (a j) -> p a j", a=2)
-                    nc.vector.tensor_copy(out=rows[:, :, 0:NBLK], in_=sc_in[q : q + 1, :, 0:NBLK])
                 nc.vector.transpose(out=sc_cols[:], in_=sc_rows[:])
             elif step == 1:
                 nc.vector.tensor_copy(out=sc_wide[:], in_=sc_cols[:, 0:1].to_broadcast([P, 32]))
@@ -376,14 +377,15 @@ def tile_lowrank_adam_style_step_d7_kernel(
                 nc.sync.dma_start(out=out_v[:, first : k + 1, :], in_=rows[:, first - base : k - base + 1, :])
 
         load_v(0, 1)
+        load_b(0, 1)
+        load_b(1, 2)
         load_a(0, 1)
         load_a(1, 2)
         load_a(2, 3)
         load_a(3, 4)
-        load_b(0, 2)
         load_mom(0, 1)
-        load_b(2, 4)
         load_mom(1, 2)
+        load_b(2, 4)
         load_mom(2, 4)
         load_v(1, 6)
         load_mom(4, 8)
@@ -394,8 +396,10 @@ def tile_lowrank_adam_style_step_d7_kernel(
         load_mom(12, 16)
         load_w(8, 16)
         inv_root(0)
-        for step in range(3):
-            spread_scales(step)
+        for c in range(CHUNKS):
+            widen_b(0, "V", slice(512 * c, 512 * (c + 1)))
+            spread_scales(c)
+        widen_b(1, "S")
         for t in range(4):
             widen_a(t)
         turn_a(0)
@@ -405,8 +409,8 @@ def tile_lowrank_adam_style_step_d7_kernel(
         turn_a(2)
         turn_a(3)
         turn_mom(-3)
-        widen_b(0, "V")
-        widen_b(1, "V")
+        widen_b(2, "V")
+        widen_b(3, "V")
         empty_a(1, 1, "S")
         empty_a(0, 1, "V")
         empty_a(2, 1, "S")
@@ -419,57 +423,54 @@ def tile_lowrank_adam_style_step_d7_kernel(
         turn_mom(-1)
         empty(-2)
         project(0)
-        widen_b(2, "V")
+        scale_b(0, range(0, 2), "V")
         quant(-2)
         project(1)
-        widen_b(3, "S", slice(1024, N))
-        empty(-1)
         inv_root(1)
+        empty(-1)
         inv_root(2)
-        widen_b(3, "V", slice(0, 1024))
+        scale_b(0, range(2, 4), "V")
         quant(-1)
-        scale_b(0, range(0, 2), "V")
+        quant_b(0)
         direction(0)
         turn_mom(0)
         turn_h(0)
         project(2)
-        scale_b(2, range(0, 2), "S")
+        scale_b(2, range(0, 3), "S")
         empty(0)
-        scale_b(0, range(2, 4), "V")
+        scale_b(1, range(0, 2), "V")
         direction(1)
         turn_mom(1)
         turn_h(1)
-        scale_b(2, range(2, 4), "S")
+        scale_b(2, range(3, 4), "S")
+        inv_root(3)
         empty(1)
-        quant_b(0)
-        scale_b(1, range(0, 2), "V")
+        scale_b(1, range(2, 4), "V")
         quant(0)
         project(3)
         lift(0, 0)
         direction(2)
         turn_mom(2)
         turn_h(2)
-        inv_root(3)
         fetch_r(3)
         empty(2)
-        scale_b(1, range(2, 4), "V")
+        quant_b(1)
         quant_b(2)
+        lift(0, 1)
         lift(0, 2)
         quant(1)
         project(4)
-        quant_b(1)
-        lift(0, 1)
         sort_mom(6, 1, 2, "V")
         direction_gpsimd(3, None)
         inv_root(4)
         finish(0, 0)
         lift(1, 0)
-        finish(0, 2)
-        lift(1, 2)
-        turn_mom(3)
-        turn_h(3)
         finish(0, 1)
         lift(1, 1)
+        turn_mom(3)
+        turn_h(3)
+        finish(0, 2)
+        lift(1, 2)
         fetch_r(4)
         sort_mom(7, 0, 1, "S")
         inv_root(5)

@@ -30,7 +30,7 @@ KIB = 1024
 MOM_AT, W_AT, V_AT = 0, 48 * KIB, 96 * KIB
 A_AT, B_AT, BG_AT = 112 * KIB, 136 * KIB, 161 * KIB
 OUT_AT = {0: A_AT, 3: B_AT, 6: MOM_AT, 11: MOM_AT + 30 * KIB}
-STORES = (0, 3, 6, 9, 11, 12, 13, 14, 15, 16)
+STORES = (0, 3, 6, 9, 10, 11, 12, 13, 14, 15, 16)
 PIECES = {}
 
 
@@ -394,7 +394,8 @@ def tile_lowrank_adam_style_step_d7_kernel(
         load_mom(8, 12)
         load_w(4, 8)
         load_mom(12, 16)
-        load_w(8, 16)
+        load_w(8, 12)
+        load_w(12, 16)
         inv_root(0)
         for c in range(CHUNKS):
             widen_b(0, "V", slice(512 * c, 512 * (c + 1)))

@@ -381,8 +381,7 @@ def tile_lowrank_adam_style_step_d7_kernel(
         load_b(1, 2)
         load_a(0, 1)
         load_a(1, 2)
-        load_a(2, 3)
-        load_a(3, 4)
+        load_a(2, 4)
         load_mom(0, 1)
         load_mom(1, 2)
         load_b(2, 4)

@@ -388,13 +388,14 @@ def tile_lowrank_adam_style_step_d7_kernel(
         load_mom(2, 4)
         load_v(1, 6)
         load_mom(4, 8)
-        load_w(0, 4)
-        load_v(6, 16)
-        load_mom(8, 12)
-        load_w(4, 8)
-        load_mom(12, 16)
-        load_w(8, 12)
-        load_w(12, 16)
+        load_w(0, 2)
+        load_mom(8, 11)
+        load_w(2, 5)
+        load_v(6, 11)
+        load_mom(11, 16)
+        load_w(5, 10)
+        load_v(11, 16)
+        load_w(10, 16)
         inv_root(0)
         for c in range(CHUNKS):
             widen_b(0, "V", slice(512 * c, 512 * (c + 1)))

from contextlib import ExitStack

import concourse.mybir as mybir
from concourse.masks import make_identity

M, N, R = 2048, 1536, 512
KEEP = 0.9

FLOPS = 2 * 2 * M * N * R

F32 = mybir.dt.float32
BF16 = mybir.dt.bfloat16
U32 = mybir.dt.uint32
U8 = mybir.dt.uint8
FP8 = mybir.dt.float8_e4m3fn
FP8X4 = mybir.dt.float8_e4m3fn_x4
ALU = mybir.AluOpType
ACT = mybir.ActivationFunctionType

P = 128
TILES = M // P
GROUPS = N // 512
NBLK = N // P
CHUNKS = N // 512
AHEAD = 3
Q_SLOTS = 3
DMA_ALIGN = 256
A_ON_VECTOR = 8
KIB = 1024
MOM_AT, W_AT, V_AT = 0, 48 * KIB, 96 * KIB
A_AT, B_AT, BG_AT = 112 * KIB, 136 * KIB, 161 * KIB
OUT_AT = {0: A_AT, 3: B_AT, 6: MOM_AT, 11: MOM_AT + 30 * KIB}
STORES = (0, 3, 6, 9, 10, 11, 12, 13, 14, 15, 16)
PIECES = {}


def tile_lowrank_adam_style_step_d7_kernel(
    tc, mom, v, w, a_bytes, a_scale, b_bytes, b_scale, out
):
    nc = tc.nc
    mom_v = mom.rearrange("(p i) k -> p i k", i=TILES)
    v_v = v.rearrange("(p i) r -> p i r", i=TILES)
    w_v = w.rearrange("(p i) n -> p i n", i=TILES)
    out_v = out.rearrange("(p i) n -> p i n", i=TILES)
    a_rows = a_bytes.rearrange("(p t) k -> p t k", t=4)
    b_rows = b_bytes.rearrange("(p t) n -> p t n", t=4)

    with ExitStack() as ctx:
        keep = ctx.enter_context(tc.tile_pool(name="keep", bufs=1))
        arena = ctx.enter_context(tc.tile_pool(name="arena", bufs=1))
        qinp = ctx.enter_context(tc.tile_pool(name="qinp", bufs=1))
        qoutp = ctx.enter_context(tc.tile_pool(name="qoutp", bufs=3))
        small = ctx.enter_context(tc.tile_pool(name="small", bufs=2))
        rsp = ctx.enter_context(tc.tile_pool(name="rsp", bufs=3))
        ps_t = ctx.enter_context(tc.psum_pool(name="ps_t", bufs=3))
        ps_r = ctx.enter_context(tc.psum_pool(name="ps_r", bufs=2))
        ps_u = ctx.enter_context(tc.psum_pool(name="ps_u", bufs=1))
        ctx.enter_context(tc.manual_schedule())

        def placed(shape, dtype, name, at):
            return arena.tile(shape, dtype, align_bytes=DMA_ALIGN, name=name, offset=at)

        sc_rows = keep.tile([P, 32], F32, align_bytes=64)
        sc_cols = keep.tile([P, 32], F32, align_bytes=64)
        sc_wide = keep.tile([P, 32], F32, align_bytes=64)
        sc_all = keep.tile([P, 32], F32, align_bytes=64)
        sc_in = keep.tile([P, 2, 16], F32, align_bytes=64)
        nc.scalar.dma_start(out=sc_in[0:P:32, 0, 0:NBLK], in_=a_scale)
        nc.scalar.dma_start(out=sc_in[0:P:32, 1, 0:NBLK], in_=b_scale)
        nc.gpsimd.memset(sc_rows[:], 0.0)

        for q in range(0, P, 32):
            rows = sc_rows[q : q + 1].rearrange("p (a j) -> p a j", a=2)
            nc.vector.tensor_copy(out=rows[:, :, 0:NBLK], in_=sc_in[q : q + 1, :, 0:NBLK])

        def spread_scales(step):
            if step == 0:
                nc.vector.transpose(out=sc_cols[:], in_=sc_rows[:])
            elif step == 1:
                nc.vector.tensor_copy(out=sc_wide[:], in_=sc_cols[:, 0:1].to_broadcast([P, 32]))
            else:
                nc.vector.transpose(out=sc_all[:], in_=sc_wide[:])

        a_sc = sc_all[:, 0:NBLK]
        b_sc = sc_all[:, 16 : 16 + NBLK]
        ident = keep.tile([P, P], F32)
        make_identity(nc, ident[:])

        mom_t, v_t, w_t, o_t = {}, {}, {}, {}
        a_b, b_b = {}, {}

        def load_planes(name, rows, at, views, t, end, pad=0):
            planes = placed([P, end - t, N + pad], U8, "%s%d" % (name, t), at + N * t)
            nc.sync.dma_start(out=planes[:, :, 0:N], in_=rows[:, t:end, :])
            for i in range(t, end):
                views[i] = planes[:, i - t, 0:N]

        def load_a(t, end):
            load_planes("a_b", a_rows, B_AT, a_b, t, end)

        def load_b(t, end, pad=0):
            load_planes("b_b", b_rows, B_AT + 6 * KIB, b_b, t, end, pad)

        def load_rows(name, src, width, at, views, k, end):
            rows = placed([P, end - k, width], BF16, "%s%d" % (name, k), at + 2 * width * k)
            nc.sync.dma_start(out=rows[:], in_=src[:, k:end, :])
            for i in range(k, end):
                views[i] = rows[:, i - k, :]

        def load_mom(k, end):
            load_rows("mom", mom_v, N, MOM_AT, mom_t, k, end)

        def load_v(k, end):
            load_rows("v", v_v, R, V_AT, v_t, k, end)

        def load_w(k, end):
            load_rows("w", w_v, N, W_AT, w_t, k, end)

        def move(eng, dst, src):
            if eng == "S":
                nc.scalar.copy(out=dst, in_=src)
            else:
                nc.vector.tensor_copy(out=dst, in_=src)

        def scaled(eng, dst, src, sc):
            if eng == "S":
                nc.scalar.activation(out=dst, in_=src, func=ACT.Copy, scale=sc)
            else:
                nc.vector.tensor_scalar(out=dst, in0=src, scalar1=sc, scalar2=None, op0=ALU.mult)

        a_wide = [placed([P, N], BF16, "a_wide%d" % t, A_AT + 3 * KIB * t) for t in range(4)]
        a_c = keep.tile([P, GROUPS, R], U32, align_bytes=64)
        a_s = keep.tile([P, GROUPS, R], U8, align_bytes=64)
        a_g, a_bank = {}, {}

        def widen_a(t):
            for j in range(NBLK):
                cols = slice(P * j, P * (j + 1))
                src = a_b[t][:, cols].bitcast(FP8)
                if j < A_ON_VECTOR:
                    g, q = divmod(j, 4)
                    dst = a_wide[t][:, 512 * g : 512 * (g + 1)].rearrange("p (x n e) -> p n x e", x=2, e=2)
                    scaled("V", dst[:, 32 * q : 32 * (q + 1)], src.rearrange("p (n x e) -> p n x e", x=2, e=2), a_sc[:, j : j + 1])
                else:
                    scaled("S", a_wide[t][:, cols], src, a_sc[:, j : j + 1])

        def turn_a(t):
            u, e = divmod(t, 2)
            words = a_wide[t][:].bitcast(F32)
            for g in range(GROUPS):
                if e == 0:
                    if u == 0:
                        a_bank[g, u] = ps_u.tile([P, 4, P], F32, name="u%d" % g)
                    elif g < 2:
                        a_bank[g, u] = ps_r.tile([P, 4, P], F32, name="r")
                    else:
                        a_bank[g, u] = ps_t.tile([P, 4, P], F32, name="bank")
                for x in range(2):
                    if 4 * g < A_ON_VECTOR:
                        src = words[:, 256 * g + P * x : 256 * g + P * (x + 1)]
                    else:
                        src = words[:, 256 * g + x : 256 * (g + 1) : 2]
                    nc.tensor.transpose(a_bank[g, u][:, 2 * e + x, :], src, ident[:])

        def empty_a(g, u, eng):
            if g not in a_g:
                a_g[g] = placed([P, 4 * R], BF16, "a_g%d" % g, A_AT + 12 * KIB + 4 * KIB * g)
            words = a_g[g][:].bitcast(F32)
            move(
                eng,
                words[:, 512 * u : 512 * (u + 1)].rearrange("p (m y) -> p m y", y=4),
                a_bank[g, u][:].rearrange("p y m -> p m y"),
            )

        def quant_a(g):
            nc.vector.quantize_mx(out=a_c[:, g, :].bitcast(FP8X4), scales=a_s[:, g, :], in_=a_g[g][:])

        b_wide = placed([P, 4, N], BF16, "b_wide", B_AT + 13 * KIB)
        b_c = keep.tile([P, N], U32, align_bytes=64)
        b_s = keep.tile([P, N], U8, align_bytes=64)
        b_g = {}

        def widen_b(t, eng, cols=slice(0, N)):
            move(eng, b_wide[:, t, cols], b_b[t][:, cols].bitcast(FP8))

        def scale_b(c, js, eng):
            if c not in b_g:
                b_g[c] = placed([P, 512, 4], BF16, "b_g%d" % c, BG_AT + 4 * KIB * c)
            for j in js:
                jj = 4 * c + j
                scaled(
                    eng,
                    b_g[c][:, P * j : P * (j + 1), :].rearrange("p (m i) t -> p m t i", i=4),
                    b_wide[:, :, P * jj : P * (jj + 1)].rearrange("p t (m i) -> p m t i", i=4),
                    b_sc[:, jj : jj + 1],
                )

        def quant_b(c):
            cols = slice(512 * c, 512 * (c + 1))
            nc.vector.quantize_mx(
                out=b_c[:, cols].bitcast(FP8X4),
                scales=b_s[:, cols],
                in_=b_g[c][:].rearrange("p n t -> p (n t)"),
            )

        srt, rs, h, r_bank, r_sb, u_bank = {}, {}, {}, {}, {}, {}
        bank_x, bank_y, q_in, q_c, q_s, u_sb, done = {}, {}, {}, {}, {}, {}, {}

        def parts(s):
            return (0 if s + AHEAD < TILES else 3), (4 if s >= 0 else 3)

        def sort_mom(k, g, n, eng):
            words = small.tile([P, n, 2, P], F32, name="srt%d" % g, bufs=3)
            src = mom_t[k].bitcast(F32)[:, 256 * g : 256 * (g + n)]
            move(eng, words[:], src.rearrange("p (g n x) -> p g x n", g=n, x=2))
            for i in range(n):
                srt[k, g + i] = words[:, i]

        def inv_root(k):
            rs[k] = rsp.tile([P, 2, P, 2], F32, name="rs")
            nc.scalar.activation(
                out=rs[k][:],
                in_=v_t[k].rearrange("p (m u e) -> p u m e", u=2, e=2),
                func=ACT.Abs_reciprocal_sqrt,
            )

        def turn_mom(s, pool=ps_t, tags=("bank", "bank")):
            k = s + AHEAD
            words = mom_t[k].bitcast(F32)
            bank_x[s] = pool.tile([P, 4, P], F32, name=tags[0])
            bank_y[s] = pool.tile([P, 4, P], F32, name=tags[1])
            for g in range(GROUPS):
                for x in range(2):
                    dst = bank_x[s][:, 2 * g + x, :] if g < 2 else bank_y[s][:, x, :]
                    if (k, g) in srt:
                        src = srt[k, g][:, x, :]
                    else:
                        src = words[:, 256 * g + x : 256 * (g + 1) : 2]
                    nc.tensor.transpose(dst, src, ident[:])

        def turn_h(s):
            if s not in bank_y:
                bank_y[s] = ps_t.tile([P, 4, P], F32, name="bank")
            words = h[s][:].bitcast(F32)
            for x in range(2):
                nc.tensor.transpose(bank_y[s][:, 2 + x, :], words[:, P * x : P * (x + 1)], ident[:])

        def empty_x(s):
            slot = s % Q_SLOTS
            q_in[s] = qinp.tile(
                [P, 4, 512], BF16, align_bytes=64, name="q_in%d" % slot, offset=4096 * slot
            )
            if parts(s)[0] == 0:
                words = q_in[s][:].bitcast(F32).rearrange("p a (n x) -> p a n x", x=2)
                nc.scalar.copy(out=words[:, 0:2], in_=bank_x[s][:].rearrange("p (a x) n -> p a n x", x=2))

        def empty_y(s):
            lo, hi = parts(s)
            lo = max(lo, 2)
            words = q_in[s][:].bitcast(F32).rearrange("p a (n x) -> p a n x", x=2)
            nc.scalar.copy(
                out=words[:, lo:hi],
                in_=bank_y[s][:].rearrange("p (a x) n -> p a n x", x=2)[:, lo - 2 : hi - 2],
            )

        def empty(s):
            empty_x(s)
            empty_y(s)

        def quant(s):
            lo, hi = parts(s)
            q_c[s] = qoutp.tile([P, 4, P], U32, align_bytes=64, name="q_c")
            q_s[s] = qoutp.tile([P, 4, P], U8, align_bytes=64, name="q_s")
            nc.vector.quantize_mx(
                out=q_c[s][:, lo:hi, :].rearrange("p a n -> p (a n)").bitcast(FP8X4),
                scales=q_s[s][:, lo:hi, :].rearrange("p a n -> p (a n)"),
                in_=q_in[s][:, lo:hi, :].rearrange("p a n -> p (a n)"),
            )

        def project(k):
            r_bank[k] = ps_r.tile([P, R], F32, name="r")
            for g in range(GROUPS):
                nc.tensor.matmul_mx(
                    out=r_bank[k][:],
                    lhsT=q_c[k - AHEAD][:, g, :].bitcast(FP8X4),
                    lhsT_scale=q_s[k - AHEAD][:, g, :],
                    rhs=a_c[:, g, :].bitcast(FP8X4),
                    rhs_scale=a_s[:, g, :],
                    start=(g == 0),
                    stop=(g == GROUPS - 1),
                )

        def direction(k):
            h[k] = small.tile([P, R], BF16, name="h")
            nc.vector.tensor_tensor(
                out=h[k][:],
                in0=r_bank[k][:],
                in1=rs[k][:].rearrange("p u m e -> p (u m e)"),
                op=ALU.mult,
            )

        def fetch_r(k):
            r_sb[k] = small.tile([P, R], F32, name="r_sb")
            nc.scalar.copy(out=r_sb[k][:], in_=r_bank[k][:])

        def direction_gpsimd(k, s):
            if s is None:
                h[k] = placed([P, R], BF16, "h_first", BG_AT + 4 * KIB)
            else:
                slot = s % Q_SLOTS
                h[k] = qinp.tile([P, R], BF16, align_bytes=64, name="h%d" % slot, offset=4096 * slot + 3072)
            nc.gpsimd.tensor_tensor(
                out=h[k][:],
                in0=r_sb[k][:],
                in1=rs[k][:].rearrange("p u m e -> p (u m e)"),
                op=ALU.mult,
            )

        def lift(k, c):
            cols = slice(512 * c, 512 * (c + 1))
            u_bank[k, c] = ps_u.tile([P, 512], F32, name="u%d" % c)
            nc.tensor.matmul_mx(
                out=u_bank[k, c][:],
                lhsT=q_c[k][:, 3, :].bitcast(FP8X4),
                lhsT_scale=q_s[k][:, 3, :],
                rhs=b_c[:, cols].bitcast(FP8X4),
                rhs_scale=b_s[:, cols],
                start=True,
                stop=True,
            )

        def out_rows(k, c):
            if k not in o_t:
                end = min([e for e in OUT_AT if e > k] + [TILES])
                rows = placed([P, end - k, N], F32, "out%d" % k, OUT_AT[k])
                for i in range(k, end):
                    o_t[i] = (rows, k)
            rows, base = o_t[k]
            return rows[:, k - base, 512 * c : 512 * (c + 1)]

        def finish(k, c):
            cols = slice(512 * c, 512 * (c + 1))
            nc.vector.scalar_tensor_tensor(
                out=out_rows(k, c),
                in0=w_t[k][:, cols],
                scalar=KEEP,
                in1=u_bank[k, c][:],
                op0=ALU.mult,
                op1=ALU.subtract,
            )
            store(k, c)

        def decay(k, c):
            nc.scalar.activation(
                out=out_rows(k, c), in_=w_t[k][:, 512 * c : 512 * (c + 1)], func=ACT.Copy, scale=KEEP
            )

        def fetch_u(k, c, s):
            slot = s % Q_SLOTS
            u_sb[k] = qinp.tile([P, 512], F32, align_bytes=64, name="u%d" % slot, offset=4096 * slot + 2048)
            nc.scalar.copy(out=u_sb[k][:], in_=u_bank[k, c][:])

        def finish_gpsimd(k, c):
            nc.gpsimd.tensor_tensor(out=out_rows(k, c), in0=out_rows(k, c), in1=u_sb[k][:], op=ALU.subtract)
            store(k, c)

        def store(k, c):
            rows, base = o_t[k]
            done.setdefault(k, set()).add(c)
            if k in PIECES:
                for lo, hi in PIECES[k]:
                    if lo <= c < hi and all(i in done[k] for i in range(lo, hi)):
                        cols = slice(512 * lo, 512 * hi)
                        nc.sync.dma_start(out=out_v[:, k, cols], in_=rows[:, k - base, cols])
            elif len(done[k]) == CHUNKS and k + 1 in STORES:
                first = STORES[STORES.index(k + 1) - 1]
                nc.sync.dma_start(out=out_v[:, first : k + 1, :], in_=rows[:, first - base : k - base + 1, :])

        load_v(0, 1)
        load_b(0, 1)
        load_b(1, 2)
        load_a(0, 1)
        load_a(1, 2)
        load_a(2, 4)
        load_mom(0, 1)
        load_mom(1, 2)
        load_b(2, 4)
        load_mom(2, 4)
        load_v(1, 6)
        load_mom(4, 8)
        load_w(0, 2)
        load_mom(8, 11)
        load_w(2, 5)
        load_v(6, 11)
        load_mom(11, 16)
        load_w(5, 10)
        load_v(11, 16)
        load_w(10, 16)
        inv_root(0)
        for c in range(CHUNKS):
            widen_b(0, "V", slice(512 * c, 512 * (c + 1)))
            spread_scales(c)
        widen_b(1, "S")
        for t in range(4):
            widen_a(t)
        turn_a(0)
        turn_a(1)
        for g in range(GROUPS):
            empty_a(g, 0, "S")
        turn_a(2)
        turn_a(3)
        turn_mom(-3)
        widen_b(2, "V")
        widen_b(3, "V")
        empty_a(1, 1, "S")
        empty_a(0, 1, "V")
        empty_a(2, 1, "S")
        turn_mom(-2, ps_u, ("u0", "u1"))
        empty(-3)
        quant_a(1)
        quant_a(0)
        quant_a(2)
        quant(-3)
        turn_mom(-1)
        empty(-2)
        project(0)
        scale_b(0, range(0, 2), "V")
        quant(-2)
        project(1)
        inv_root(1)
        empty(-1)
        inv_root(2)
        scale_b(0, range(2, 4), "V")
        quant(-1)
        quant_b(0)
        direction(0)
        turn_mom(0)
        turn_h(0)
        project(2)
        scale_b(2, range(0, 3), "S")
        empty(0)
        scale_b(1, range(0, 2), "V")
        direction(1)
        turn_mom(1)
        turn_h(1)
        scale_b(2, range(3, 4), "S")
        inv_root(3)
        empty(1)
        scale_b(1, range(2, 4), "V")
        quant(0)
        project(3)
        lift(0, 0)
        direction(2)
        turn_mom(2)
        turn_h(2)
        fetch_r(3)
        empty(2)
        quant_b(1)
        quant_b(2)
        lift(0, 1)
        lift(0, 2)
        quant(1)
        project(4)
        sort_mom(6, 1, 2, "V")
        direction_gpsimd(3, None)
        inv_root(4)
        finish(0, 0)
        lift(1, 0)
        finish(0, 1)
        lift(1, 1)
        turn_mom(3)
        turn_h(3)
        finish(0, 2)
        lift(1, 2)
        fetch_r(4)
        sort_mom(7, 0, 1, "S")
        inv_root(5)
        empty(3)

        def on_gpsimd(k):
            return 4 <= k < TILES and (True)

        for s in range(2, TILES + 1):
            late = s + AHEAD > TILES
            if late:
                finish(s - 1, 0)
            if s < TILES:
                quant(s)
            if s + 2 + AHEAD < TILES:
                sort_mom(s + 2 + AHEAD, 3 - 2, 2, "V")
            if s + AHEAD < TILES:
                project(s + AHEAD)
            if on_gpsimd(s + 2):
                direction_gpsimd(s + 2, s)
            elif s + 2 < TILES:
                direction(s + 2)
            for c in range(CHUNKS):
                if c == 2:
                    if s + 3 + AHEAD < TILES:
                        sort_mom(s + 3 + AHEAD, 0, 1, "S")
                    if on_gpsimd(s + 3):
                        fetch_r(s + 3)
                    if s + 4 < TILES:
                        inv_root(s + 4)
                    if s + 2 + AHEAD < TILES:
                        turn_mom(s + 2)
                    if s + 2 < TILES:
                        turn_h(s + 2)
                        empty(s + 2)
                if c > 0 or not late:
                    finish(s - 1, c)
                if s < TILES:
                    lift(s, c)
